import numpy as np
import ml_dtypes


def mxq(x, axis, fmt="e4m3"):
    dtype, down = {"e4m3": (ml_dtypes.float8_e4m3fn, 7), "e5m2": (ml_dtypes.float8_e5m2, 14)}[fmt]
    v = np.moveaxis(np.asarray(x, np.float32).astype(ml_dtypes.bfloat16).astype(np.float64), axis, -1)
    blocks = v.reshape(v.shape[:-1] + (-1, 32))
    amax = np.abs(blocks).max(-1, keepdims=True)
    byte = np.maximum(np.where(amax > 0, np.frexp(amax)[1] - 1 + 127, 0) - down, 1)
    scale = np.exp2(byte - 127.0)
    codes = (blocks / scale).astype(np.float32).astype(dtype).astype(np.float64)
    return np.moveaxis((codes * scale).reshape(v.shape), -1, axis)


WIDE = False


def mx_kscale(k):
    if not WIDE:
        return np.ones(k)
    levels = np.array([10, -10, 5, -5, 0])
    if k % 512:
        return np.exp2(np.random.permutation(np.resize(levels, k // 32))).repeat(32)
    a = np.empty((k // 512, 16))
    for p in range(k // 512):
        a[p, :8] = np.random.permutation(np.resize(levels, 8))
        for g in range(8):
            far = levels[np.abs(levels - a[p, g]) >= 10]
            a[p, g + 8] = far[np.random.randint(len(far))]
    return np.exp2(a.ravel()).repeat(32)


def f64(x):
    return np.asarray(x).astype(np.float64)


def striped(idx):
    return np.tile(np.asarray(idx).reshape(-1, 16).T, (8, 1)).astype(np.uint16)


def unstriped(offs):
    return offs[:16].T.reshape(-1).astype(np.int64)


def striped8(idx):
    return np.asarray(idx).reshape(8, -1, 16).transpose(0, 2, 1).reshape(128, -1).astype(np.uint16)


def unstriped8(offs):
    return offs.reshape(8, 16, -1).transpose(0, 2, 1).reshape(8, -1).astype(np.int64)


def pick8(x, idx, run):
    r = np.arange(len(x))
    return x[r[:, None], idx[r % (8 * run) // run]]


E2M1 = np.array([0.0, 0.5, 1.0, 1.5, 2.0, 3.0, 4.0, 6.0, -0.0, -0.5, -1.0, -1.5, -2.0, -3.0, -4.0, -6.0])


def pack_weight(w, fmt):
    k, n = w.shape
    w = f64(np.asarray(w, np.float32).astype(ml_dtypes.bfloat16)).reshape(k // 32, 32, n)
    amax = np.abs(w).max(1)
    if fmt == "e4m3":
        byte = np.frexp(amax)[1] - 1 + 127 - 7
    else:
        mant, ex = np.frexp(amax / 6.0)
        byte = np.where(mant > 0.5, ex, ex - 1) + 127
    byte = np.clip(np.where(amax > 0, byte, 1), 1, 254)
    scaled = (w * np.exp2(127.0 - byte)[:, None, :]).reshape(k, n).astype(np.float32)
    by_word = np.ascontiguousarray(scaled.reshape(k // 512, 128, 4, n).transpose(0, 1, 3, 2))
    if fmt == "e4m3":
        words = by_word.astype(ml_dtypes.float8_e4m3fn).view(np.uint8)
    else:
        c = by_word.astype(ml_dtypes.float4_e2m1fn).view(np.uint8) & 0xF
        words = (c[..., 0::2] | (c[..., 1::2] << 4)).reshape(k // 512, 128, 2 * n)
    return np.ascontiguousarray(words), np.ascontiguousarray(byte.astype(np.uint8).reshape(k // 512, 16, n))


def unpack_weight(words, scales, fmt):
    g, _, n = scales.shape
    words = np.ascontiguousarray(words).reshape(g, 128, n, -1)
    if fmt == "e4m3":
        vals = words.view(ml_dtypes.float8_e4m3fn).astype(np.float64)
    else:
        nib = np.empty((g, 128, n, 4), np.uint8)
        nib[..., 0::2] = words & 0xF
        nib[..., 1::2] = words >> 4
        vals = E2M1[nib]
    vals = vals * np.repeat(np.exp2(scales.astype(np.float64) - 127.0), 8, axis=1)[..., None]
    return vals.transpose(0, 1, 3, 2).reshape(g * 512, n)


K, U, I, T, E = 512, 2048, 512, 1024, 512


def setup_inputs():
    n = np.random.standard_normal
    idx = np.random.permutation(U)[:I]
    idx2 = np.stack([np.random.permutation(T)[:I] for _ in range(8)])
    fk = mx_kscale(K)
    embp = pack_weight(n((K, U)) / fk[:, None], "e4m3")
    return {
        "emb_words": embp[0],
        "emb_scales": embp[1],
        "wv": (n((K, E)) * 1 / np.sqrt(K) * fk[:, None]).astype(np.float32),
        "old": (n((E, T))).astype(np.float32),
        "retain": (np.random.uniform(0.0, 1.0, (1, T))).astype(np.float32),
        "offs": striped(idx),
        "offs2": striped8(idx2),
    }


def reference(emb_words, emb_scales, wv, old, retain, offs, offs2):
    idx = unstriped(offs)
    idx2 = unstriped8(offs2)
    embu = unpack_weight(emb_words, emb_scales, "e4m3")
    wvq = mxq(f64(wv), 0, "e4m3")
    embidxg = embu[:, idx]
    v = wvq.T @ embidxg
    vf = np.zeros((E, T))
    vf[np.arange(E)[:, None], idx2[np.arange(E) % 512 // 64]] = v
    y = f64(old) * f64(retain) + vf
    return y

@@ -1,0 +1,157 @@
+from contextlib import ExitStack
+
+import concourse.mybir as mybir
+from concourse.masks import make_identity
+
+K, U, I, T, E = 512, 2048, 512, 1024, 512
+FLOPS = 2 * K * E * I
+
+F32 = mybir.dt.float32
+BF16 = mybir.dt.bfloat16
+I32 = mybir.dt.int32
+U32 = mybir.dt.uint32
+U16 = mybir.dt.uint16
+U8 = mybir.dt.uint8
+FP8X4 = mybir.dt.float8_e4m3fn_x4
+COPY = mybir.ActivationFunctionType.Copy
+ADD = mybir.AluOpType.add
+MULT = mybir.AluOpType.mult
+
+P = 128
+PACK = 4
+TILES = E // P
+BANK = 512
+BLOCKS = T // P
+HALVES = T // BANK
+PER_BANK = BANK // P
+
+
+def tile_attend_headwrite_kernel(tc, emb_words, emb_scales, wv, old, retain, offs, offs2, out):
+    nc = tc.nc
+    with ExitStack() as ctx:
+        keep = ctx.enter_context(tc.tile_pool(name="keep", bufs=1))
+        psum = ctx.enter_context(tc.psum_pool(name="psum", bufs=1))
+        banks = [psum.tile([P, BANK], F32, name="bank%d" % n) for n in range(8)]
+
+        emb_list = keep.tile([P, I // 16], U16, name="emb_list")
+        place_list = keep.tile([P, I // 16], U16, name="place_list")
+        wv_raw = keep.tile([P, PACK, E], F32, name="wv_raw", tag="slot_b")
+        words = keep.tile([P, U], U32, name="words")
+        scales = keep.tile([P, U], U8, name="scales")
+        retain_rows = keep.tile([P, P], F32, name="retain_rows", tag="slot_a")
+
+        nc.vector.memset(scales[:].bitcast(I32), 0)
+        nc.gpsimd.memset(retain_rows[:], 0.0)
+
+        nc.sync.dma_start(emb_list[:], offs)
+        nc.sync.dma_start(out=wv_raw[:], in_=wv.rearrange("(p r) e -> p r e", r=PACK))
+        nc.sync.dma_start(out=words[:].bitcast(I32), in_=emb_words[0].rearrange("p n r -> p (n r)").bitcast(I32))
+        nc.sync.dma_start(place_list[:], offs2)
+        for q in range(4):
+            nc.scalar.dma_start(
+                out=scales[32 * q : 32 * q + 4, :].bitcast(I32),
+                in_=emb_scales[0, 4 * q : 4 * q + 4, :].bitcast(I32),
+            )
+        nc.scalar.dma_start(out=retain_rows[0:BLOCKS, :], in_=retain.rearrange("o (b q) -> (o b) q", q=P))
+        old_view = old.rearrange("(p j) t -> p j t", j=TILES)
+        out_view = out.rearrange("(p j) t -> p j t", j=TILES)
+
+        ident = keep.tile([P, P], F32, name="ident")
+        make_identity(nc, ident[:])
+
+        windows = [keep.tile([P, T], F32, name="window%d" % j) for j in range(TILES)]
+        for j in range(TILES):
+            nc.vector.memset(windows[j][:], 0.0)
+
+        retain_cols = keep.tile([P, BLOCKS], F32, name="retain_cols")
+        nc.tensor.transpose(banks[7][:, 0:P], retain_rows[:], ident[:])
+        nc.scalar.copy(retain_cols[:], banks[7][:, 0:BLOCKS])
+        old_first = keep.tile([P, T], F32, name="old_first", tag="slot_a")
+        nc.sync.dma_start(out=old_first[:], in_=old_view[:, 0, :])
+
+        picked_scales = keep.tile([P, I], U8, name="picked_scales", align_bytes=64)
+        nc.vector.tensor_copy(picked_scales[:], scales[:].indirect(emb_list[:]))
+
+        wv_bf = keep.tile([P, TILES, P, PACK], BF16, name="wv_bf", align_bytes=64, tag="slot_c")
+        dealt = wv_bf[:].rearrange("p j m r -> p m r j")
+        source = wv_raw[:].rearrange("p r (m j) -> p m r j", j=TILES)
+        split = P // 2
+        nc.vector.tensor_copy(out=dealt[:, 0:split], in_=source[:, 0:split])
+        nc.scalar.copy(out=dealt[:, split:P], in_=source[:, split:P])
+        old_middle = keep.tile([P, 2, T], F32, name="old_middle", tag="slot_b")
+        nc.sync.dma_start(out=old_middle[:], in_=old_view[:, 1:3, :])
+
+        wv_codes = keep.tile([P, E], U32, name="wv_codes", align_bytes=64)
+        wv_scales = keep.tile([P, E], U8, name="wv_scales", align_bytes=64)
+        nc.vector.quantize_mx(
+            out=wv_codes[:].bitcast(FP8X4),
+            scales=wv_scales[:],
+            in_=wv_bf[:].rearrange("p j m r -> p (j m r)"),
+        )
+        old_last = keep.tile([P, T], F32, name="old_last", align_bytes=64, tag="slot_c")
+        nc.sync.dma_start(out=old_last[:], in_=old_view[:, 3, :])
+        old_sb = [old_first[:], old_middle[:, 0, :], old_middle[:, 1, :], old_last[:]]
+
+        retain_all = keep.tile([P, T], F32, name="retain_all")
+        for h in range(HALVES):
+            for c in range(PER_BANK):
+                b = h * PER_BANK + c
+                nc.tensor.transpose(
+                    banks[5 + h][:, c * P : (c + 1) * P], retain_cols[:, b : b + 1].to_broadcast([P, P]), ident[:]
+                )
+            nc.scalar.copy(retain_all[:, h * BANK : (h + 1) * BANK], banks[5 + h][:])
+
+        picked_words = keep.tile([P, I], U32, name="picked_words", align_bytes=64)
+        half = I // 2
+        for s in range(2):
+            nc.vector.tensor_copy(
+                picked_words[:, s * half : (s + 1) * half],
+                words[:].indirect(emb_list[:, s * half // 16 : (s + 1) * half // 16]),
+            )
+
+        pieces = [(0, 0, half), (0, half, I)] + [(j, 0, I) for j in range(1, TILES)]
+        values = [keep.tile([P, I], F32, name="values%d" % j) for j in range(TILES)]
+        for n, (j, lo, hi) in enumerate(pieces):
+            nc.tensor.matmul_mx(
+                out=banks[n][:, 0 : hi - lo],
+                lhsT=wv_codes[:, j * P : (j + 1) * P].bitcast(FP8X4),
+                lhsT_scale=wv_scales[:, j * P : (j + 1) * P],
+                rhs=picked_words[:, lo:hi].bitcast(FP8X4),
+                rhs_scale=picked_scales[:, lo:hi],
+                start=True,
+                stop=True,
+            )
+            nc.scalar.copy(values[j][:, lo:hi], banks[n][:, 0 : hi - lo])
+        for j, lo, hi in pieces:
+            nc.vector.tensor_copy(windows[j][:].indirect(place_list[:, lo // 16 : hi // 16]), values[j][:, lo:hi])
+
+        kept = [keep.tile([P, T], F32, name="kept%d" % j) for j in range(3)]
+        for j in range(2):
+            nc.gpsimd.tensor_tensor(kept[j][:], old_sb[j], retain_all[:], MULT)
+
+        kept_t = [keep.tile([P, 2, P], F32, name="kept_t%d" % b) for b in range(BLOCKS)]
+        for b in range(BLOCKS):
+            bank = banks[5 + b % 3]
+            for j in range(2):
+                nc.tensor.transpose(bank[:, j * P : (j + 1) * P], old_sb[2 + j][:, b * P : (b + 1) * P], ident[:])
+            nc.scalar.activation(
+                kept_t[b][:].rearrange("q j p -> q (j p)"), bank[:, 0 : 2 * P], COPY, scale=retain_cols[:, b : b + 1]
+            )
+        for j in range(2):
+            for h in range(HALVES):
+                for c in range(PER_BANK):
+                    nc.tensor.transpose(
+                        banks[2 * j + h][:, c * P : (c + 1) * P], kept_t[h * PER_BANK + c][:, j, :], ident[:]
+                    )
+        for h in range(HALVES):
+            nc.scalar.copy(kept[2][:, h * BANK : (h + 1) * BANK], banks[h][:])
+
+        for j in range(3):
+            result = keep.tile([P, T], F32, name="result%d" % j)
+            nc.gpsimd.tensor_tensor(result[:], kept[j][:], windows[j][:], ADD)
+            nc.sync.dma_start(out=out_view[:, j, :], in_=result[:])
+
+        for h in range(HALVES):
+            cols = slice(h * BANK, (h + 1) * BANK)
+            nc.vector.tensor_tensor(kept[2][:, cols], banks[2 + h][:], windows[3][:, cols], ADD)
+            nc.sync.dma_start(out=out_view[:, 3, cols], in_=kept[2][:, cols])

@@ -38,21 +38,21 @@ def tile_attend_headwrite_kernel(tc, emb_words, emb_scales, wv, old, retain, off
         wv_raw = keep.tile([P, PACK, E], F32, name="wv_raw", tag="slot_b")
         words = keep.tile([P, U], U32, name="words")
         scales = keep.tile([P, U], U8, name="scales")
-        retain_rows = keep.tile([P, P], F32, name="retain_rows", tag="slot_a")
+        retain_rows = keep.tile([P, P], F32, name="retain_rows")
 
         nc.vector.memset(scales[:].bitcast(I32), 0)
         nc.gpsimd.memset(retain_rows[:], 0.0)
 
         nc.sync.dma_start(emb_list[:], offs)
         nc.sync.dma_start(out=wv_raw[:], in_=wv.rearrange("(p r) e -> p r e", r=PACK))
-        nc.sync.dma_start(out=words[:].bitcast(I32), in_=emb_words[0].rearrange("p n r -> p (n r)").bitcast(I32))
-        nc.sync.dma_start(place_list[:], offs2)
         for q in range(4):
-            nc.scalar.dma_start(
+            nc.sync.dma_start(
                 out=scales[32 * q : 32 * q + 4, :].bitcast(I32),
                 in_=emb_scales[0, 4 * q : 4 * q + 4, :].bitcast(I32),
             )
-        nc.scalar.dma_start(out=retain_rows[0:BLOCKS, :], in_=retain.rearrange("o (b q) -> (o b) q", q=P))
+        nc.sync.dma_start(out=retain_rows[0:BLOCKS, :], in_=retain.rearrange("o (b q) -> (o b) q", q=P))
+        nc.sync.dma_start(out=words[:].bitcast(I32), in_=emb_words[0].rearrange("p n r -> p (n r)").bitcast(I32))
+        nc.sync.dma_start(place_list[:], offs2)
         old_view = old.rearrange("(p j) t -> p j t", j=TILES)
         out_view = out.rearrange("(p j) t -> p j t", j=TILES)
 
@@ -66,8 +66,6 @@ def tile_attend_headwrite_kernel(tc, emb_words, emb_scales, wv, old, retain, off
         retain_cols = keep.tile([P, BLOCKS], F32, name="retain_cols")
         nc.tensor.transpose(banks[7][:, 0:P], retain_rows[:], ident[:])
         nc.scalar.copy(retain_cols[:], banks[7][:, 0:BLOCKS])
-        old_first = keep.tile([P, T], F32, name="old_first", tag="slot_a")
-        nc.sync.dma_start(out=old_first[:], in_=old_view[:, 0, :])
 
         picked_scales = keep.tile([P, I], U8, name="picked_scales", align_bytes=64)
         nc.vector.tensor_copy(picked_scales[:], scales[:].indirect(emb_list[:]))
@@ -78,8 +76,9 @@ def tile_attend_headwrite_kernel(tc, emb_words, emb_scales, wv, old, retain, off
         split = P // 2
         nc.vector.tensor_copy(out=dealt[:, 0:split], in_=source[:, 0:split])
         nc.scalar.copy(out=dealt[:, split:P], in_=source[:, split:P])
-        old_middle = keep.tile([P, 2, T], F32, name="old_middle", tag="slot_b")
-        nc.sync.dma_start(out=old_middle[:], in_=old_view[:, 1:3, :])
+        old_low = keep.tile([P, 2, T], F32, name="old_low", tag="slot_b")
+        for j in range(2):
+            nc.sync.dma_start(out=old_low[:, j, :], in_=old_view[:, j, :])
 
         wv_codes = keep.tile([P, E], U32, name="wv_codes", align_bytes=64)
         wv_scales = keep.tile([P, E], U8, name="wv_scales", align_bytes=64)
@@ -88,9 +87,10 @@ def tile_attend_headwrite_kernel(tc, emb_words, emb_scales, wv, old, retain, off
             scales=wv_scales[:],
             in_=wv_bf[:].rearrange("p j m r -> p (j m r)"),
         )
-        old_last = keep.tile([P, T], F32, name="old_last", align_bytes=64, tag="slot_c")
-        nc.sync.dma_start(out=old_last[:], in_=old_view[:, 3, :])
-        old_sb = [old_first[:], old_middle[:, 0, :], old_middle[:, 1, :], old_last[:]]
+        old_high = keep.tile([P, 2, T], F32, name="old_high", align_bytes=64, tag="slot_c")
+        for j in range(2):
+            nc.sync.dma_start(out=old_high[:, j, :], in_=old_view[:, 2 + j, :])
+        old_sb = [old_low[:, 0, :], old_low[:, 1, :], old_high[:, 0, :], old_high[:, 1, :]]
 
         retain_all = keep.tile([P, T], F32, name="retain_all")
         for h in range(HALVES):

@@ -35,16 +35,16 @@ def tile_attend_headwrite_kernel(tc, emb_words, emb_scales, wv, old, retain, off
 
         emb_list = keep.tile([P, I // 16], U16, name="emb_list")
         place_list = keep.tile([P, I // 16], U16, name="place_list")
-        wv_raw = keep.tile([P, PACK, E], F32, name="wv_raw", tag="slot_b")
-        words = keep.tile([P, U], U32, name="words")
-        scales = keep.tile([P, U], U8, name="scales")
+        wv_raw = keep.tile([P, PACK, E], F32, name="wv_raw")
+        words = keep.tile([P, U], U32, name="words", tag="words_then_codes", align_bytes=64)
+        scales = keep.tile([P, U], U8, name="scales", tag="scales_then_codes", align_bytes=64)
         retain_rows = keep.tile([P, P], F32, name="retain_rows")
 
         nc.vector.memset(scales[:].bitcast(I32), 0)
         nc.gpsimd.memset(retain_rows[:], 0.0)
 
-        nc.sync.dma_start(emb_list[:], offs)
         nc.sync.dma_start(out=wv_raw[:], in_=wv.rearrange("(p r) e -> p r e", r=PACK))
+        nc.sync.dma_start(emb_list[:], offs)
         for q in range(4):
             nc.sync.dma_start(
                 out=scales[32 * q : 32 * q + 4, :].bitcast(I32),
@@ -55,13 +55,17 @@ def tile_attend_headwrite_kernel(tc, emb_words, emb_scales, wv, old, retain, off
         nc.sync.dma_start(place_list[:], offs2)
         old_view = old.rearrange("(p j) t -> p j t", j=TILES)
         out_view = out.rearrange("(p j) t -> p j t", j=TILES)
+        old_sb = [keep.tile([P, T], F32, name="old%d" % j) for j in range(TILES)]
+        for j in range(TILES):
+            nc.sync.dma_start(out=old_sb[j][:], in_=old_view[:, j, :])
 
         ident = keep.tile([P, P], F32, name="ident")
         make_identity(nc, ident[:])
 
         windows = [keep.tile([P, T], F32, name="window%d" % j) for j in range(TILES)]
-        for j in range(TILES):
+        for j in range(TILES - 1):
             nc.vector.memset(windows[j][:], 0.0)
+        nc.gpsimd.memset(windows[TILES - 1][:], 0.0)
 
         retain_cols = keep.tile([P, BLOCKS], F32, name="retain_cols")
         nc.tensor.transpose(banks[7][:, 0:P], retain_rows[:], ident[:])
@@ -70,27 +74,28 @@ def tile_attend_headwrite_kernel(tc, emb_words, emb_scales, wv, old, retain, off
         picked_scales = keep.tile([P, I], U8, name="picked_scales", align_bytes=64)
         nc.vector.tensor_copy(picked_scales[:], scales[:].indirect(emb_list[:]))
 
-        wv_bf = keep.tile([P, TILES, P, PACK], BF16, name="wv_bf", align_bytes=64, tag="slot_c")
-        dealt = wv_bf[:].rearrange("p j m r -> p m r j")
+        pair = TILES // 2
         source = wv_raw[:].rearrange("p r (m j) -> p m r j", j=TILES)
-        split = P // 2
-        nc.vector.tensor_copy(out=dealt[:, 0:split], in_=source[:, 0:split])
-        nc.scalar.copy(out=dealt[:, split:P], in_=source[:, split:P])
-        old_low = keep.tile([P, 2, T], F32, name="old_low", tag="slot_b")
-        for j in range(2):
-            nc.sync.dma_start(out=old_low[:, j, :], in_=old_view[:, j, :])
+        wv_bf = [keep.tile([P, pair, P, PACK], BF16, name="wv_bf%d" % g, align_bytes=64) for g in range(2)]
+        nc.vector.tensor_copy(out=wv_bf[0][:].rearrange("p j m r -> p m r j"), in_=source[:, :, :, 0:pair])
+        nc.scalar.copy(out=wv_bf[1][:].rearrange("p j m r -> p m r j"), in_=source[:, :, :, pair:TILES])
 
-        wv_codes = keep.tile([P, E], U32, name="wv_codes", align_bytes=64)
-        wv_scales = keep.tile([P, E], U8, name="wv_scales", align_bytes=64)
-        nc.vector.quantize_mx(
-            out=wv_codes[:].bitcast(FP8X4),
-            scales=wv_scales[:],
-            in_=wv_bf[:].rearrange("p j m r -> p (j m r)"),
-        )
-        old_high = keep.tile([P, 2, T], F32, name="old_high", align_bytes=64, tag="slot_c")
-        for j in range(2):
-            nc.sync.dma_start(out=old_high[:, j, :], in_=old_view[:, 2 + j, :])
-        old_sb = [old_low[:, 0, :], old_low[:, 1, :], old_high[:, 0, :], old_high[:, 1, :]]
+        wv_codes = []
+        wv_scales = []
+
+        def quantize_pair(g, tag):
+            codes = keep.tile([P, pair * P], U32, name="wv_codes%d" % g, tag=tag, align_bytes=64)
+            plane = keep.tile([P, pair * P], U8, name="wv_scales%d" % g, align_bytes=64)
+            nc.vector.quantize_mx(
+                out=codes[:].bitcast(FP8X4),
+                scales=plane[:],
+                in_=wv_bf[g][:].rearrange("p j m r -> p (j m r)"),
+            )
+            for j in range(pair):
+                wv_codes.append(codes[:, j * P : (j + 1) * P])
+                wv_scales.append(plane[:, j * P : (j + 1) * P])
+
+        quantize_pair(0, "scales_then_codes")
 
         retain_all = keep.tile([P, T], F32, name="retain_all")
         for h in range(HALVES):
@@ -108,30 +113,33 @@ def tile_attend_headwrite_kernel(tc, emb_words, emb_scales, wv, old, retain, off
                 picked_words[:, s * half : (s + 1) * half],
                 words[:].indirect(emb_list[:, s * half // 16 : (s + 1) * half // 16]),
             )
+        quantize_pair(1, "words_then_codes")
 
-        pieces = [(0, 0, half), (0, half, I)] + [(j, 0, I) for j in range(1, TILES)]
+        products = [(0, 0, P), (1, 0, half), (0, P, half), (0, half, I), (1, half, I), (2, 0, I), (3, 0, I)]
+        scatters = [(0, 0, P), (1, 0, half), (0, P, I), (1, half, I), (2, 0, I), (3, 0, I)]
+        product_banks = [banks[n] for n in (0, 1, 2, 3, 4, 7, 5)]
         values = [keep.tile([P, I], F32, name="values%d" % j) for j in range(TILES)]
-        for n, (j, lo, hi) in enumerate(pieces):
+        for n, (j, lo, hi) in enumerate(products):
             nc.tensor.matmul_mx(
-                out=banks[n][:, 0 : hi - lo],
-                lhsT=wv_codes[:, j * P : (j + 1) * P].bitcast(FP8X4),
-                lhsT_scale=wv_scales[:, j * P : (j + 1) * P],
+                out=product_banks[n][:, 0 : hi - lo],
+                lhsT=wv_codes[j].bitcast(FP8X4),
+                lhsT_scale=wv_scales[j],
                 rhs=picked_words[:, lo:hi].bitcast(FP8X4),
                 rhs_scale=picked_scales[:, lo:hi],
                 start=True,
                 stop=True,
             )
-            nc.scalar.copy(values[j][:, lo:hi], banks[n][:, 0 : hi - lo])
-        for j, lo, hi in pieces:
+            nc.scalar.copy(values[j][:, lo:hi], product_banks[n][:, 0 : hi - lo])
+        for j, lo, hi in scatters:
             nc.vector.tensor_copy(windows[j][:].indirect(place_list[:, lo // 16 : hi // 16]), values[j][:, lo:hi])
 
         kept = [keep.tile([P, T], F32, name="kept%d" % j) for j in range(3)]
         for j in range(2):
-            nc.gpsimd.tensor_tensor(kept[j][:], old_sb[j], retain_all[:], MULT)
+            nc.gpsimd.tensor_tensor(kept[j][:], old_sb[j][:], retain_all[:], MULT)
 
         kept_t = [keep.tile([P, 2, P], F32, name="kept_t%d" % b) for b in range(BLOCKS)]
         for b in range(BLOCKS):
-            bank = banks[5 + b % 3]
+            bank = banks[4 + b % 4]
             for j in range(2):
                 nc.tensor.transpose(bank[:, j * P : (j + 1) * P], old_sb[2 + j][:, b * P : (b + 1) * P], ident[:])
             nc.scalar.activation(
@@ -146,12 +154,18 @@ def tile_attend_headwrite_kernel(tc, emb_words, emb_scales, wv, old, retain, off
         for h in range(HALVES):
             nc.scalar.copy(kept[2][:, h * BANK : (h + 1) * BANK], banks[h][:])
 
-        for j in range(3):
-            result = keep.tile([P, T], F32, name="result%d" % j)
+        for j in range(2):
+            result = old_sb[1 - j]
             nc.gpsimd.tensor_tensor(result[:], kept[j][:], windows[j][:], ADD)
             nc.sync.dma_start(out=out_view[:, j, :], in_=result[:])
-
         for h in range(HALVES):
             cols = slice(h * BANK, (h + 1) * BANK)
-            nc.vector.tensor_tensor(kept[2][:, cols], banks[2 + h][:], windows[3][:, cols], ADD)
+            nc.gpsimd.tensor_tensor(old_sb[2][:, cols], kept[2][:, cols], windows[2][:, cols], ADD)
+            nc.scalar.dma_start(out=out_view[:, 2, cols], in_=old_sb[2][:, cols])
+
+        piece = BANK // 2
+        for lo in range(0, T, piece):
+            h, c = divmod(lo, BANK)
+            cols = slice(lo, lo + piece)
+            nc.vector.tensor_tensor(kept[2][:, cols], banks[2 + h][:, c : c + piece], windows[3][:, cols], ADD)
             nc.sync.dma_start(out=out_view[:, 3, cols], in_=kept[2][:, cols])

@@ -45,10 +45,10 @@ def tile_attend_headwrite_kernel(tc, emb_words, emb_scales, wv, old, retain, off
 
         nc.sync.dma_start(out=wv_raw[:], in_=wv.rearrange("(p r) e -> p r e", r=PACK))
         nc.sync.dma_start(emb_list[:], offs)
-        for q in range(4):
+        for r in range(4):
             nc.sync.dma_start(
-                out=scales[32 * q : 32 * q + 4, :].bitcast(I32),
-                in_=emb_scales[0, 4 * q : 4 * q + 4, :].bitcast(I32),
+                out=scales[r:P:32, :].bitcast(I32),
+                in_=emb_scales[0, r:16:4, :].bitcast(I32),
             )
         nc.sync.dma_start(out=retain_rows[0:BLOCKS, :], in_=retain.rearrange("o (b q) -> (o b) q", q=P))
         nc.sync.dma_start(out=words[:].bitcast(I32), in_=emb_words[0].rearrange("p n r -> p (n r)").bitcast(I32))
@@ -76,7 +76,9 @@ def tile_attend_headwrite_kernel(tc, emb_words, emb_scales, wv, old, retain, off
 
         pair = TILES // 2
         source = wv_raw[:].rearrange("p r (m j) -> p m r j", j=TILES)
-        wv_bf = [keep.tile([P, pair, P, PACK], BF16, name="wv_bf%d" % g, align_bytes=64) for g in range(2)]
+        wv_bf = [
+            keep.tile([P, pair, P, PACK], BF16, name="wv_bf%d" % g, tag="wv_bf%d" % g, align_bytes=64) for g in range(2)
+        ]
         nc.vector.tensor_copy(out=wv_bf[0][:].rearrange("p j m r -> p m r j"), in_=source[:, :, :, 0:pair])
         nc.scalar.copy(out=wv_bf[1][:].rearrange("p j m r -> p m r j"), in_=source[:, :, :, pair:TILES])
 
@@ -133,7 +135,11 @@ def tile_attend_headwrite_kernel(tc, emb_words, emb_scales, wv, old, retain, off
         for j, lo, hi in scatters:
             nc.vector.tensor_copy(windows[j][:].indirect(place_list[:, lo // 16 : hi // 16]), values[j][:, lo:hi])
 
-        kept = [keep.tile([P, T], F32, name="kept%d" % j) for j in range(3)]
+        kept = [
+            keep.tile([P, T], F32, name="kept0", tag="wv_bf1", align_bytes=64),
+            keep.tile([P, T], F32, name="kept1"),
+            keep.tile([P, T], F32, name="kept2"),
+        ]
         for j in range(2):
             nc.gpsimd.tensor_tensor(kept[j][:], old_sb[j][:], retain_all[:], MULT)
 

@@ -24,6 +24,8 @@ BANK = 512
 BLOCKS = T // P
 HALVES = T // BANK
 PER_BANK = BANK // P
+WV_FIRST = 1280
+VECTOR_COLUMNS = 64
 
 
 def tile_attend_headwrite_kernel(tc, emb_words, emb_scales, wv, old, retain, offs, offs2, out):
@@ -35,22 +37,27 @@ def tile_attend_headwrite_kernel(tc, emb_words, emb_scales, wv, old, retain, off
 
         emb_list = keep.tile([P, I // 16], U16, name="emb_list")
         place_list = keep.tile([P, I // 16], U16, name="place_list")
-        wv_raw = keep.tile([P, PACK, E], F32, name="wv_raw")
-        words = keep.tile([P, U], U32, name="words", tag="words_then_codes", align_bytes=64)
-        scales = keep.tile([P, U], U8, name="scales", tag="scales_then_codes", align_bytes=64)
-        retain_rows = keep.tile([P, P], F32, name="retain_rows")
+        wv_raw = keep.tile([P, PACK, E], F32, name="wv_raw", tag="wv_raw")
+        words = keep.tile([P, U], U32, name="words")
+        scales = keep.tile([P, U], U8, name="scales", tag="wv_bf0", align_bytes=64)
+        retain_rows = keep.tile([P, P], F32, name="retain_rows", tag="wv_bf1", align_bytes=64)
 
+        ident = keep.tile([P, P], F32, name="ident")
         nc.vector.memset(scales[:].bitcast(I32), 0)
-        nc.gpsimd.memset(retain_rows[:], 0.0)
+        nc.vector.memset(retain_rows[:], 0.0)
+        nc.vector.memset(ident[:], 0.0)
 
-        nc.sync.dma_start(out=wv_raw[:], in_=wv.rearrange("(p r) e -> p r e", r=PACK))
+        wv_rows = wv.rearrange("(p r) e -> p (r e)", r=PACK)
+        wv_flat = wv_raw[:].rearrange("p r e -> p (r e)")
         nc.sync.dma_start(emb_list[:], offs)
+        nc.sync.dma_start(out=wv_flat[:, 0:WV_FIRST], in_=wv_rows[:, 0:WV_FIRST])
         for r in range(4):
             nc.sync.dma_start(
                 out=scales[r:P:32, :].bitcast(I32),
                 in_=emb_scales[0, r:16:4, :].bitcast(I32),
             )
         nc.sync.dma_start(out=retain_rows[0:BLOCKS, :], in_=retain.rearrange("o (b q) -> (o b) q", q=P))
+        nc.sync.dma_start(out=wv_flat[:, WV_FIRST:], in_=wv_rows[:, WV_FIRST:])
         nc.sync.dma_start(out=words[:].bitcast(I32), in_=emb_words[0].rearrange("p n r -> p (n r)").bitcast(I32))
         nc.sync.dma_start(place_list[:], offs2)
         old_view = old.rearrange("(p j) t -> p j t", j=TILES)
@@ -59,13 +66,12 @@ def tile_attend_headwrite_kernel(tc, emb_words, emb_scales, wv, old, retain, off
         for j in range(TILES):
             nc.sync.dma_start(out=old_sb[j][:], in_=old_view[:, j, :])
 
-        ident = keep.tile([P, P], F32, name="ident")
-        make_identity(nc, ident[:])
+        make_identity(nc, ident[:], nomemset=True)
 
-        windows = [keep.tile([P, T], F32, name="window%d" % j) for j in range(TILES)]
-        for j in range(TILES - 1):
-            nc.vector.memset(windows[j][:], 0.0)
-        nc.gpsimd.memset(windows[TILES - 1][:], 0.0)
+        windows = [keep.tile([P, T], F32, name="window%d" % j) for j in range(TILES - 1)]
+        for window in windows[:2]:
+            nc.vector.memset(window[:].bitcast(I32), 0)
+        nc.gpsimd.memset(windows[2][:], 0.0)
 
         retain_cols = keep.tile([P, BLOCKS], F32, name="retain_cols")
         nc.tensor.transpose(banks[7][:, 0:P], retain_rows[:], ident[:])
@@ -80,13 +86,15 @@ def tile_attend_headwrite_kernel(tc, emb_words, emb_scales, wv, old, retain, off
             keep.tile([P, pair, P, PACK], BF16, name="wv_bf%d" % g, tag="wv_bf%d" % g, align_bytes=64) for g in range(2)
         ]
         nc.vector.tensor_copy(out=wv_bf[0][:].rearrange("p j m r -> p m r j"), in_=source[:, :, :, 0:pair])
-        nc.scalar.copy(out=wv_bf[1][:].rearrange("p j m r -> p m r j"), in_=source[:, :, :, pair:TILES])
+        second = wv_bf[1][:].rearrange("p j m r -> p m r j")
+        nc.vector.tensor_copy(out=second[:, 0:VECTOR_COLUMNS], in_=source[:, 0:VECTOR_COLUMNS, :, pair:TILES])
+        nc.scalar.copy(out=second[:, VECTOR_COLUMNS:P], in_=source[:, VECTOR_COLUMNS:P, :, pair:TILES])
 
         wv_codes = []
         wv_scales = []
 
-        def quantize_pair(g, tag):
-            codes = keep.tile([P, pair * P], U32, name="wv_codes%d" % g, tag=tag, align_bytes=64)
+        def quantize_pair(g):
+            codes = keep.tile([P, pair * P], U32, name="wv_codes%d" % g, align_bytes=64)
             plane = keep.tile([P, pair * P], U8, name="wv_scales%d" % g, align_bytes=64)
             nc.vector.quantize_mx(
                 out=codes[:].bitcast(FP8X4),
@@ -97,9 +105,10 @@ def tile_attend_headwrite_kernel(tc, emb_words, emb_scales, wv, old, retain, off
                 wv_codes.append(codes[:, j * P : (j + 1) * P])
                 wv_scales.append(plane[:, j * P : (j + 1) * P])
 
-        quantize_pair(0, "scales_then_codes")
+        quantize_pair(0)
+        quantize_pair(1)
 
-        retain_all = keep.tile([P, T], F32, name="retain_all")
+        retain_all = keep.tile([P, T], F32, name="retain_all", tag="wv_raw")
         for h in range(HALVES):
             for c in range(PER_BANK):
                 b = h * PER_BANK + c
@@ -108,14 +117,13 @@ def tile_attend_headwrite_kernel(tc, emb_words, emb_scales, wv, old, retain, off
                 )
             nc.scalar.copy(retain_all[:, h * BANK : (h + 1) * BANK], banks[5 + h][:])
 
-        picked_words = keep.tile([P, I], U32, name="picked_words", align_bytes=64)
+        picked_words = keep.tile([P, I], U32, name="picked_words", tag="wv_bf1", align_bytes=64)
         half = I // 2
         for s in range(2):
             nc.vector.tensor_copy(
                 picked_words[:, s * half : (s + 1) * half],
                 words[:].indirect(emb_list[:, s * half // 16 : (s + 1) * half // 16]),
             )
-        quantize_pair(1, "words_then_codes")
 
         products = [(0, 0, P), (1, 0, half), (0, P, half), (0, half, I), (1, half, I), (2, 0, I), (3, 0, I)]
         scatters = [(0, 0, P), (1, 0, half), (0, P, I), (1, half, I), (2, 0, I), (3, 0, I)]
@@ -132,11 +140,11 @@ def tile_attend_headwrite_kernel(tc, emb_words, emb_scales, wv, old, retain, off
                 stop=True,
             )
             nc.scalar.copy(values[j][:, lo:hi], product_banks[n][:, 0 : hi - lo])
-        for j, lo, hi in scatters:
+        for j, lo, hi in scatters[:-1]:
             nc.vector.tensor_copy(windows[j][:].indirect(place_list[:, lo // 16 : hi // 16]), values[j][:, lo:hi])
 
         kept = [
-            keep.tile([P, T], F32, name="kept0", tag="wv_bf1", align_bytes=64),
+            keep.tile([P, T], F32, name="kept0"),
             keep.tile([P, T], F32, name="kept1"),
             keep.tile([P, T], F32, name="kept2"),
         ]
@@ -164,6 +172,7 @@ def tile_attend_headwrite_kernel(tc, emb_words, emb_scales, wv, old, retain, off
             result = old_sb[1 - j]
             nc.gpsimd.tensor_tensor(result[:], kept[j][:], windows[j][:], ADD)
             nc.sync.dma_start(out=out_view[:, j, :], in_=result[:])
+        nc.vector.tensor_copy(windows[0][:].indirect(place_list[:]), values[3][:])
         for h in range(HALVES):
             cols = slice(h * BANK, (h + 1) * BANK)
             nc.gpsimd.tensor_tensor(old_sb[2][:, cols], kept[2][:, cols], windows[2][:, cols], ADD)
@@ -173,5 +182,5 @@ def tile_attend_headwrite_kernel(tc, emb_words, emb_scales, wv, old, retain, off
         for lo in range(0, T, piece):
             h, c = divmod(lo, BANK)
             cols = slice(lo, lo + piece)
-            nc.vector.tensor_tensor(kept[2][:, cols], banks[2 + h][:, c : c + piece], windows[3][:, cols], ADD)
+            nc.vector.tensor_tensor(kept[2][:, cols], banks[2 + h][:, c : c + piece], windows[0][:, cols], ADD)
             nc.sync.dma_start(out=out_view[:, 3, cols], in_=kept[2][:, cols])

@@ -24,7 +24,9 @@ BANK = 512
 BLOCKS = T // P
 HALVES = T // BANK
 PER_BANK = BANK // P
-WV_FIRST = 1280
+SCALE_ROWS = 16
+SPREAD = P // SCALE_ROWS
+WV_FIRST = 1024
 VECTOR_COLUMNS = 64
 
 
@@ -32,6 +34,7 @@ def tile_attend_headwrite_kernel(tc, emb_words, emb_scales, wv, old, retain, off
     nc = tc.nc
     with ExitStack() as ctx:
         keep = ctx.enter_context(tc.tile_pool(name="keep", bufs=1))
+        turns = ctx.enter_context(tc.tile_pool(name="turns", bufs=1))
         psum = ctx.enter_context(tc.psum_pool(name="psum", bufs=1))
         banks = [psum.tile([P, BANK], F32, name="bank%d" % n) for n in range(8)]
 
@@ -39,27 +42,32 @@ def tile_attend_headwrite_kernel(tc, emb_words, emb_scales, wv, old, retain, off
         place_list = keep.tile([P, I // 16], U16, name="place_list")
         wv_raw = keep.tile([P, PACK, E], F32, name="wv_raw", tag="wv_raw")
         words = keep.tile([P, U], U32, name="words")
-        scales = keep.tile([P, U], U8, name="scales", tag="wv_bf0", align_bytes=64)
-        retain_rows = keep.tile([P, P], F32, name="retain_rows", tag="wv_bf1", align_bytes=64)
-
+        scales = turns.tile([P, U], U8, name="scales", offset=0, align_bytes=64)
+        retain_rows = turns.tile([P, P], F32, name="retain_rows", offset=U, align_bytes=64)
         ident = keep.tile([P, P], F32, name="ident")
+        picked_scales = keep.tile([P, I], U8, name="picked_scales", align_bytes=64)
+        plane = keep.tile([P, I], U8, name="plane", align_bytes=64)
+
         nc.vector.memset(scales[:].bitcast(I32), 0)
         nc.vector.memset(retain_rows[:], 0.0)
         nc.vector.memset(ident[:], 0.0)
 
         wv_rows = wv.rearrange("(p r) e -> p (r e)", r=PACK)
         wv_flat = wv_raw[:].rearrange("p r e -> p (r e)")
-        nc.sync.dma_start(emb_list[:], offs)
+        word_rows = emb_words[0].rearrange("p n r -> p (n r)").bitcast(I32)
         nc.sync.dma_start(out=wv_flat[:, 0:WV_FIRST], in_=wv_rows[:, 0:WV_FIRST])
-        for r in range(4):
-            nc.sync.dma_start(
-                out=scales[r:P:32, :].bitcast(I32),
-                in_=emb_scales[0, r:16:4, :].bitcast(I32),
-            )
+        nc.sync.dma_start(emb_list[:], offs)
+        nc.sync.dma_start(out=scales[0:P:SPREAD, :].bitcast(I32), in_=emb_scales[0].bitcast(I32))
         nc.sync.dma_start(out=retain_rows[0:BLOCKS, :], in_=retain.rearrange("o (b q) -> (o b) q", q=P))
         nc.sync.dma_start(out=wv_flat[:, WV_FIRST:], in_=wv_rows[:, WV_FIRST:])
-        nc.sync.dma_start(out=words[:].bitcast(I32), in_=emb_words[0].rearrange("p n r -> p (n r)").bitcast(I32))
+        nc.sync.dma_start(out=words[:].bitcast(I32), in_=word_rows)
         nc.sync.dma_start(place_list[:], offs2)
+
+        nc.vector.tensor_copy(picked_scales[:], scales[:].indirect(emb_list[:]))
+        for r in range(4):
+            nc.sync.dma_start(
+                out=plane[r:P:32, :].bitcast(I32), in_=picked_scales[r * SPREAD : P : 32, :].bitcast(I32)
+            )
         old_view = old.rearrange("(p j) t -> p j t", j=TILES)
         out_view = out.rearrange("(p j) t -> p j t", j=TILES)
         old_sb = [keep.tile([P, T], F32, name="old%d" % j) for j in range(TILES)]
@@ -77,36 +85,23 @@ def tile_attend_headwrite_kernel(tc, emb_words, emb_scales, wv, old, retain, off
         nc.tensor.transpose(banks[7][:, 0:P], retain_rows[:], ident[:])
         nc.scalar.copy(retain_cols[:], banks[7][:, 0:BLOCKS])
 
-        picked_scales = keep.tile([P, I], U8, name="picked_scales", align_bytes=64)
-        nc.vector.tensor_copy(picked_scales[:], scales[:].indirect(emb_list[:]))
-
         pair = TILES // 2
         source = wv_raw[:].rearrange("p r (m j) -> p m r j", j=TILES)
-        wv_bf = [
-            keep.tile([P, pair, P, PACK], BF16, name="wv_bf%d" % g, tag="wv_bf%d" % g, align_bytes=64) for g in range(2)
-        ]
-        nc.vector.tensor_copy(out=wv_bf[0][:].rearrange("p j m r -> p m r j"), in_=source[:, :, :, 0:pair])
-        second = wv_bf[1][:].rearrange("p j m r -> p m r j")
-        nc.vector.tensor_copy(out=second[:, 0:VECTOR_COLUMNS], in_=source[:, 0:VECTOR_COLUMNS, :, pair:TILES])
-        nc.scalar.copy(out=second[:, VECTOR_COLUMNS:P], in_=source[:, VECTOR_COLUMNS:P, :, pair:TILES])
+        wv_bf = turns.tile([P, TILES, P, PACK], BF16, name="wv_bf", offset=0, align_bytes=64)
+        dealt = wv_bf[:].rearrange("p j m r -> p m r j")
+        nc.vector.tensor_copy(out=dealt[:, :, :, 0:pair], in_=source[:, :, :, 0:pair])
+        nc.vector.tensor_copy(out=dealt[:, 0:VECTOR_COLUMNS, :, pair:], in_=source[:, 0:VECTOR_COLUMNS, :, pair:])
+        nc.scalar.copy(out=dealt[:, VECTOR_COLUMNS:, :, pair:], in_=source[:, VECTOR_COLUMNS:, :, pair:])
 
-        wv_codes = []
-        wv_scales = []
-
-        def quantize_pair(g):
-            codes = keep.tile([P, pair * P], U32, name="wv_codes%d" % g, align_bytes=64)
-            plane = keep.tile([P, pair * P], U8, name="wv_scales%d" % g, align_bytes=64)
+        wv_codes = keep.tile([P, E], U32, name="wv_codes", align_bytes=64)
+        wv_scales = keep.tile([P, E], U8, name="wv_scales", align_bytes=64)
+        for g in range(2):
+            cols = slice(g * pair * P, (g + 1) * pair * P)
             nc.vector.quantize_mx(
-                out=codes[:].bitcast(FP8X4),
-                scales=plane[:],
-                in_=wv_bf[g][:].rearrange("p j m r -> p (j m r)"),
+                out=wv_codes[:, cols].bitcast(FP8X4),
+                scales=wv_scales[:, cols],
+                in_=wv_bf[:, g * pair : (g + 1) * pair].rearrange("p j m r -> p (j m r)"),
             )
-            for j in range(pair):
-                wv_codes.append(codes[:, j * P : (j + 1) * P])
-                wv_scales.append(plane[:, j * P : (j + 1) * P])
-
-        quantize_pair(0)
-        quantize_pair(1)
 
         retain_all = keep.tile([P, T], F32, name="retain_all", tag="wv_raw")
         for h in range(HALVES):
@@ -117,7 +112,7 @@ def tile_attend_headwrite_kernel(tc, emb_words, emb_scales, wv, old, retain, off
                 )
             nc.scalar.copy(retain_all[:, h * BANK : (h + 1) * BANK], banks[5 + h][:])
 
-        picked_words = keep.tile([P, I], U32, name="picked_words", tag="wv_bf1", align_bytes=64)
+        picked_words = turns.tile([P, I], U32, name="picked_words", offset=0, align_bytes=64)
         half = I // 2
         for s in range(2):
             nc.vector.tensor_copy(
@@ -126,28 +121,24 @@ def tile_attend_headwrite_kernel(tc, emb_words, emb_scales, wv, old, retain, off
             )
 
         products = [(0, 0, P), (1, 0, half), (0, P, half), (0, half, I), (1, half, I), (2, 0, I), (3, 0, I)]
-        scatters = [(0, 0, P), (1, 0, half), (0, P, I), (1, half, I), (2, 0, I), (3, 0, I)]
+        scatters = [(0, 0, P), (1, 0, half), (0, P, I), (1, half, I), (2, 0, I)]
         product_banks = [banks[n] for n in (0, 1, 2, 3, 4, 7, 5)]
         values = [keep.tile([P, I], F32, name="values%d" % j) for j in range(TILES)]
         for n, (j, lo, hi) in enumerate(products):
             nc.tensor.matmul_mx(
                 out=product_banks[n][:, 0 : hi - lo],
-                lhsT=wv_codes[j].bitcast(FP8X4),
-                lhsT_scale=wv_scales[j],
+                lhsT=wv_codes[:, j * P : (j + 1) * P].bitcast(FP8X4),
+                lhsT_scale=wv_scales[:, j * P : (j + 1) * P],
                 rhs=picked_words[:, lo:hi].bitcast(FP8X4),
-                rhs_scale=picked_scales[:, lo:hi],
+                rhs_scale=plane[:, lo:hi],
                 start=True,
                 stop=True,
             )
             nc.scalar.copy(values[j][:, lo:hi], product_banks[n][:, 0 : hi - lo])
-        for j, lo, hi in scatters[:-1]:
+        for j, lo, hi in scatters:
             nc.vector.tensor_copy(windows[j][:].indirect(place_list[:, lo // 16 : hi // 16]), values[j][:, lo:hi])
 
-        kept = [
-            keep.tile([P, T], F32, name="kept0"),
-            keep.tile([P, T], F32, name="kept1"),
-            keep.tile([P, T], F32, name="kept2"),
-        ]
+        kept = [keep.tile([P, T], F32, name="kept%d" % j) for j in range(3)]
         for j in range(2):
             nc.gpsimd.tensor_tensor(kept[j][:], old_sb[j][:], retain_all[:], MULT)
 
@@ -182,5 +173,5 @@ def tile_attend_headwrite_kernel(tc, emb_words, emb_scales, wv, old, retain, off
         for lo in range(0, T, piece):
             h, c = divmod(lo, BANK)
             cols = slice(lo, lo + piece)
-            nc.vector.tensor_tensor(kept[2][:, cols], banks[2 + h][:, c : c + piece], windows[0][:, cols], ADD)
-            nc.sync.dma_start(out=out_view[:, 3, cols], in_=kept[2][:, cols])
+            nc.vector.tensor_tensor(kept[1][:, cols], banks[2 + h][:, c : c + piece], windows[0][:, cols], ADD)
+            nc.sync.dma_start(out=out_view[:, 3, cols], in_=kept[1][:, cols])

@@ -1,7 +1,6 @@
 from contextlib import ExitStack
 
 import concourse.mybir as mybir
-from concourse.masks import make_identity
 
 K, U, I, T, E = 512, 2048, 512, 1024, 512
 FLOPS = 2 * K * E * I
@@ -50,7 +49,8 @@ def tile_attend_headwrite_kernel(tc, emb_words, emb_scales, wv, old, retain, off
 
         nc.vector.memset(scales[:].bitcast(I32), 0)
         nc.vector.memset(retain_rows[:], 0.0)
-        nc.vector.memset(ident[:], 0.0)
+        zeros = keep.tile([P, P], F32, name="zeros", tag="window2")
+        nc.vector.memset(zeros[:], 0.0)
 
         wv_rows = wv.rearrange("(p r) e -> p (r e)", r=PACK)
         wv_flat = wv_raw[:].rearrange("p r e -> p (r e)")
@@ -74,9 +74,17 @@ def tile_attend_headwrite_kernel(tc, emb_words, emb_scales, wv, old, retain, off
         for j in range(TILES):
             nc.sync.dma_start(out=old_sb[j][:], in_=old_view[:, j, :])
 
-        make_identity(nc, ident[:], nomemset=True)
+        nc.gpsimd.affine_select(
+            out=ident[:],
+            in_=zeros[:],
+            compare_op=mybir.AluOpType.not_equal,
+            fill=1.0,
+            base=0,
+            pattern=[[-1, P]],
+            channel_multiplier=1,
+        )
 
-        windows = [keep.tile([P, T], F32, name="window%d" % j) for j in range(TILES - 1)]
+        windows = [keep.tile([P, T], F32, name="window%d" % j, tag="window%d" % j) for j in range(TILES - 1)]
         for window in windows[:2]:
             nc.vector.memset(window[:].bitcast(I32), 0)
         nc.gpsimd.memset(windows[2][:], 0.0)

@@ -25,7 +25,7 @@ HALVES = T // BANK
 PER_BANK = BANK // P
 SCALE_ROWS = 16
 SPREAD = P // SCALE_ROWS
-WV_FIRST = 1024
+WV_FIRST = 768
 VECTOR_COLUMNS = 64
 
 
@@ -49,6 +49,9 @@ def tile_attend_headwrite_kernel(tc, emb_words, emb_scales, wv, old, retain, off
 
         nc.vector.memset(scales[:].bitcast(I32), 0)
         nc.vector.memset(retain_rows[:], 0.0)
+        windows = [keep.tile([P, T], F32, name="window%d" % j) for j in range(2)]
+        for window in windows:
+            nc.vector.memset(window[:].bitcast(I32), 0)
         zeros = keep.tile([P, P], F32, name="zeros", tag="window2")
         nc.vector.memset(zeros[:], 0.0)
 
@@ -84,9 +87,7 @@ def tile_attend_headwrite_kernel(tc, emb_words, emb_scales, wv, old, retain, off
             channel_multiplier=1,
         )
 
-        windows = [keep.tile([P, T], F32, name="window%d" % j, tag="window%d" % j) for j in range(TILES - 1)]
-        for window in windows[:2]:
-            nc.vector.memset(window[:].bitcast(I32), 0)
+        windows.append(keep.tile([P, T], F32, name="window2", tag="window2"))
         nc.gpsimd.memset(windows[2][:], 0.0)
 
         retain_cols = keep.tile([P, BLOCKS], F32, name="retain_cols")

@@ -26,7 +26,8 @@ PER_BANK = BANK // P
 SCALE_ROWS = 16
 SPREAD = P // SCALE_ROWS
 WV_FIRST = 768
-VECTOR_COLUMNS = 64
+EARLY = 3
+LAST_OFFSET = EARLY * P * PACK * 2
 
 
 def tile_attend_headwrite_kernel(tc, emb_words, emb_scales, wv, old, retain, offs, offs2, out):
@@ -42,7 +43,7 @@ def tile_attend_headwrite_kernel(tc, emb_words, emb_scales, wv, old, retain, off
         wv_raw = keep.tile([P, PACK, E], F32, name="wv_raw", tag="wv_raw")
         words = keep.tile([P, U], U32, name="words")
         scales = turns.tile([P, U], U8, name="scales", offset=0, align_bytes=64)
-        retain_rows = turns.tile([P, P], F32, name="retain_rows", offset=U, align_bytes=64)
+        retain_rows = turns.tile([P, P], F32, name="retain_rows", offset=LAST_OFFSET, align_bytes=64)
         ident = keep.tile([P, P], F32, name="ident")
         picked_scales = keep.tile([P, I], U8, name="picked_scales", align_bytes=64)
         plane = keep.tile([P, I], U8, name="plane", align_bytes=64)
@@ -94,23 +95,24 @@ def tile_attend_headwrite_kernel(tc, emb_words, emb_scales, wv, old, retain, off
         nc.tensor.transpose(banks[7][:, 0:P], retain_rows[:], ident[:])
         nc.scalar.copy(retain_cols[:], banks[7][:, 0:BLOCKS])
 
-        pair = TILES // 2
         source = wv_raw[:].rearrange("p r (m j) -> p m r j", j=TILES)
-        wv_bf = turns.tile([P, TILES, P, PACK], BF16, name="wv_bf", offset=0, align_bytes=64)
-        dealt = wv_bf[:].rearrange("p j m r -> p m r j")
-        nc.vector.tensor_copy(out=dealt[:, :, :, 0:pair], in_=source[:, :, :, 0:pair])
-        nc.vector.tensor_copy(out=dealt[:, 0:VECTOR_COLUMNS, :, pair:], in_=source[:, 0:VECTOR_COLUMNS, :, pair:])
-        nc.scalar.copy(out=dealt[:, VECTOR_COLUMNS:, :, pair:], in_=source[:, VECTOR_COLUMNS:, :, pair:])
+        early_bf = turns.tile([P, EARLY, P, PACK], BF16, name="early_bf", offset=0, align_bytes=64)
+        last_bf = turns.tile([P, P, PACK], BF16, name="last_bf", offset=LAST_OFFSET, align_bytes=64)
+        nc.vector.tensor_copy(out=early_bf[:].rearrange("p j m r -> p m r j"), in_=source[:, :, :, 0:EARLY])
+        nc.scalar.copy(out=last_bf[:], in_=source[:, :, :, EARLY])
 
         wv_codes = keep.tile([P, E], U32, name="wv_codes", align_bytes=64)
         wv_scales = keep.tile([P, E], U8, name="wv_scales", align_bytes=64)
-        for g in range(2):
-            cols = slice(g * pair * P, (g + 1) * pair * P)
-            nc.vector.quantize_mx(
-                out=wv_codes[:, cols].bitcast(FP8X4),
-                scales=wv_scales[:, cols],
-                in_=wv_bf[:, g * pair : (g + 1) * pair].rearrange("p j m r -> p (j m r)"),
-            )
+        nc.vector.quantize_mx(
+            out=wv_codes[:, 0 : EARLY * P].bitcast(FP8X4),
+            scales=wv_scales[:, 0 : EARLY * P],
+            in_=early_bf[:].rearrange("p j m r -> p (j m r)"),
+        )
+        nc.vector.quantize_mx(
+            out=wv_codes[:, EARLY * P :].bitcast(FP8X4),
+            scales=wv_scales[:, EARLY * P :],
+            in_=last_bf[:].rearrange("p m r -> p (m r)"),
+        )
 
         retain_all = keep.tile([P, T], F32, name="retain_all", tag="wv_raw")
         for h in range(HALVES):
@@ -147,7 +149,8 @@ def tile_attend_headwrite_kernel(tc, emb_words, emb_scales, wv, old, retain, off
         for j, lo, hi in scatters:
             nc.vector.tensor_copy(windows[j][:].indirect(place_list[:, lo // 16 : hi // 16]), values[j][:, lo:hi])
 
-        kept = [keep.tile([P, T], F32, name="kept%d" % j) for j in range(3)]
+        kept = [turns.tile([P, T], F32, name="kept0", offset=LAST_OFFSET, align_bytes=64)]
+        kept.extend(keep.tile([P, T], F32, name="kept%d" % j) for j in range(1, 3))
         for j in range(2):
             nc.gpsimd.tensor_tensor(kept[j][:], old_sb[j][:], retain_all[:], MULT)
 

@@ -25,6 +25,7 @@ HALVES = T // BANK
 PER_BANK = BANK // P
 SCALE_ROWS = 16
 SPREAD = P // SCALE_ROWS
+FIRST = 128
 WV_FIRST = 768
 EARLY = 3
 LAST_OFFSET = EARLY * P * PACK * 2
@@ -124,29 +125,26 @@ def tile_attend_headwrite_kernel(tc, emb_words, emb_scales, wv, old, retain, off
             nc.scalar.copy(retain_all[:, h * BANK : (h + 1) * BANK], banks[5 + h][:])
 
         picked_words = turns.tile([P, I], U32, name="picked_words", offset=0, align_bytes=64)
-        half = I // 2
-        for s in range(2):
-            nc.vector.tensor_copy(
-                picked_words[:, s * half : (s + 1) * half],
-                words[:].indirect(emb_list[:, s * half // 16 : (s + 1) * half // 16]),
-            )
+        for lo, hi in ((0, FIRST), (FIRST, I)):
+            nc.vector.tensor_copy(picked_words[:, lo:hi], words[:].indirect(emb_list[:, lo // 16 : hi // 16]))
 
-        products = [(0, 0, P), (1, 0, half), (0, P, half), (0, half, I), (1, half, I), (2, 0, I), (3, 0, I)]
-        scatters = [(0, 0, P), (1, 0, half), (0, P, I), (1, half, I), (2, 0, I)]
-        product_banks = [banks[n] for n in (0, 1, 2, 3, 4, 7, 5)]
+        pieces = [(0, 0, FIRST), (1, 0, FIRST), (0, FIRST, I), (1, FIRST, I), (2, 0, I), (3, 0, I)]
+        product_banks = [banks[n] for n in (0, 1, 2, 3, 4, 7)]
         values = [keep.tile([P, I], F32, name="values%d" % j) for j in range(TILES)]
-        for n, (j, lo, hi) in enumerate(products):
-            nc.tensor.matmul_mx(
-                out=product_banks[n][:, 0 : hi - lo],
-                lhsT=wv_codes[:, j * P : (j + 1) * P].bitcast(FP8X4),
-                lhsT_scale=wv_scales[:, j * P : (j + 1) * P],
-                rhs=picked_words[:, lo:hi].bitcast(FP8X4),
-                rhs_scale=plane[:, lo:hi],
-                start=True,
-                stop=True,
-            )
+        for n, (j, lo, hi) in enumerate(pieces):
+            cuts = [lo, 2 * FIRST, hi] if lo == FIRST else [lo, hi]
+            for a, b in zip(cuts, cuts[1:]):
+                nc.tensor.matmul_mx(
+                    out=product_banks[n][:, a - lo : b - lo],
+                    lhsT=wv_codes[:, j * P : (j + 1) * P].bitcast(FP8X4),
+                    lhsT_scale=wv_scales[:, j * P : (j + 1) * P],
+                    rhs=picked_words[:, a:b].bitcast(FP8X4),
+                    rhs_scale=plane[:, a:b],
+                    start=True,
+                    stop=True,
+                )
             nc.scalar.copy(values[j][:, lo:hi], product_banks[n][:, 0 : hi - lo])
-        for j, lo, hi in scatters:
+        for j, lo, hi in pieces[:-1]:
             nc.vector.tensor_copy(windows[j][:].indirect(place_list[:, lo // 16 : hi // 16]), values[j][:, lo:hi])
 
         kept = [turns.tile([P, T], F32, name="kept0", offset=LAST_OFFSET, align_bytes=64)]

@@ -66,13 +66,13 @@ def tile_attend_headwrite_kernel(tc, emb_words, emb_scales, wv, old, retain, off
         nc.sync.dma_start(out=retain_rows[0:BLOCKS, :], in_=retain.rearrange("o (b q) -> (o b) q", q=P))
         nc.sync.dma_start(out=wv_flat[:, WV_FIRST:], in_=wv_rows[:, WV_FIRST:])
         nc.sync.dma_start(out=words[:].bitcast(I32), in_=word_rows)
-        nc.sync.dma_start(place_list[:], offs2)
 
         nc.vector.tensor_copy(picked_scales[:], scales[:].indirect(emb_list[:]))
         for r in range(4):
             nc.sync.dma_start(
                 out=plane[r:P:32, :].bitcast(I32), in_=picked_scales[r * SPREAD : P : 32, :].bitcast(I32)
             )
+        nc.sync.dma_start(place_list[:], offs2)
         old_view = old.rearrange("(p j) t -> p j t", j=TILES)
         out_view = out.rearrange("(p j) t -> p j t", j=TILES)
         old_sb = [keep.tile([P, T], F32, name="old%d" % j) for j in range(TILES)]
@@ -148,7 +148,7 @@ def tile_attend_headwrite_kernel(tc, emb_words, emb_scales, wv, old, retain, off
             nc.vector.tensor_copy(windows[j][:].indirect(place_list[:, lo // 16 : hi // 16]), values[j][:, lo:hi])
 
         kept = [turns.tile([P, T], F32, name="kept0", offset=LAST_OFFSET, align_bytes=64)]
-        kept.extend(keep.tile([P, T], F32, name="kept%d" % j) for j in range(1, 3))
+        kept.extend(keep.tile([P, T], F32, name="kept%d" % j, tag="kept%d" % j) for j in range(1, 3))
         for j in range(2):
             nc.gpsimd.tensor_tensor(kept[j][:], old_sb[j][:], retain_all[:], MULT)
 
@@ -160,12 +160,15 @@ def tile_attend_headwrite_kernel(tc, emb_words, emb_scales, wv, old, retain, off
             nc.scalar.activation(
                 kept_t[b][:].rearrange("q j p -> q (j p)"), bank[:, 0 : 2 * P], COPY, scale=retain_cols[:, b : b + 1]
             )
-        for j in range(2):
+        for j in (1, 0):
             for h in range(HALVES):
                 for c in range(PER_BANK):
                     nc.tensor.transpose(
                         banks[2 * j + h][:, c * P : (c + 1) * P], kept_t[h * PER_BANK + c][:, j, :], ident[:]
                     )
+        kept_last = keep.tile([P, 256], F32, name="kept_last")
+        nc.scalar.copy(kept_last[:, 0:192], banks[2][:, 320:])
+        nc.scalar.copy(kept_last[:, 192:], banks[3][:, 0:64])
         for h in range(HALVES):
             nc.scalar.copy(kept[2][:, h * BANK : (h + 1) * BANK], banks[h][:])
 
@@ -179,9 +182,9 @@ def tile_attend_headwrite_kernel(tc, emb_words, emb_scales, wv, old, retain, off
             nc.gpsimd.tensor_tensor(old_sb[2][:, cols], kept[2][:, cols], windows[2][:, cols], ADD)
             nc.scalar.dma_start(out=out_view[:, 2, cols], in_=old_sb[2][:, cols])
 
-        piece = BANK // 2
-        for lo in range(0, T, piece):
-            h, c = divmod(lo, BANK)
-            cols = slice(lo, lo + piece)
-            nc.vector.tensor_tensor(kept[1][:, cols], banks[2 + h][:, c : c + piece], windows[0][:, cols], ADD)
-            nc.sync.dma_start(out=out_view[:, 3, cols], in_=kept[1][:, cols])
+        sums = keep.tile([P, T], F32, name="sums", tag="kept2")
+        nc.gpsimd.tensor_tensor(sums[:, 320:576], kept_last[:], windows[0][:, 320:576], ADD)
+        for start, lo, hi in ((0, 0, 128), (128, 128, 320), (320, 576, 704), (704, 704, 1024)):
+            h, col = divmod(lo, BANK)
+            nc.vector.tensor_tensor(sums[:, lo:hi], banks[2 + h][:, col : col + hi - lo], windows[0][:, lo:hi], ADD)
+            nc.sync.dma_start(out=out_view[:, 3, start:hi], in_=sums[:, start:hi])

@@ -28,7 +28,9 @@ SPREAD = P // SCALE_ROWS
 FIRST = 128
 WV_FIRST = 768
 EARLY = 3
-LAST_OFFSET = EARLY * P * PACK * 2
+SHARE = 256
+EARLY_OFFSET = T * 4
+OLD_OFFSET = EARLY_OFFSET + I * 4
 
 
 def tile_attend_headwrite_kernel(tc, emb_words, emb_scales, wv, old, retain, offs, offs2, out):
@@ -43,8 +45,8 @@ def tile_attend_headwrite_kernel(tc, emb_words, emb_scales, wv, old, retain, off
         place_list = keep.tile([P, I // 16], U16, name="place_list")
         wv_raw = keep.tile([P, PACK, E], F32, name="wv_raw", tag="wv_raw")
         words = keep.tile([P, U], U32, name="words")
-        scales = turns.tile([P, U], U8, name="scales", offset=0, align_bytes=64)
-        retain_rows = turns.tile([P, P], F32, name="retain_rows", offset=LAST_OFFSET, align_bytes=64)
+        scales = turns.tile([P, U], U8, name="scales", offset=EARLY_OFFSET, align_bytes=64)
+        retain_rows = turns.tile([P, P], F32, name="retain_rows", offset=0, align_bytes=64)
         ident = keep.tile([P, P], F32, name="ident")
         picked_scales = keep.tile([P, I], U8, name="picked_scales", align_bytes=64)
         plane = keep.tile([P, I], U8, name="plane", align_bytes=64)
@@ -73,11 +75,6 @@ def tile_attend_headwrite_kernel(tc, emb_words, emb_scales, wv, old, retain, off
                 out=plane[r:P:32, :].bitcast(I32), in_=picked_scales[r * SPREAD : P : 32, :].bitcast(I32)
             )
         nc.sync.dma_start(place_list[:], offs2)
-        old_view = old.rearrange("(p j) t -> p j t", j=TILES)
-        out_view = out.rearrange("(p j) t -> p j t", j=TILES)
-        old_sb = [keep.tile([P, T], F32, name="old%d" % j) for j in range(TILES)]
-        for j in range(TILES):
-            nc.sync.dma_start(out=old_sb[j][:], in_=old_view[:, j, :])
 
         nc.gpsimd.affine_select(
             out=ident[:],
@@ -97,8 +94,8 @@ def tile_attend_headwrite_kernel(tc, emb_words, emb_scales, wv, old, retain, off
         nc.scalar.copy(retain_cols[:], banks[7][:, 0:BLOCKS])
 
         source = wv_raw[:].rearrange("p r (m j) -> p m r j", j=TILES)
-        early_bf = turns.tile([P, EARLY, P, PACK], BF16, name="early_bf", offset=0, align_bytes=64)
-        last_bf = turns.tile([P, P, PACK], BF16, name="last_bf", offset=LAST_OFFSET, align_bytes=64)
+        early_bf = turns.tile([P, EARLY, P, PACK], BF16, name="early_bf", offset=EARLY_OFFSET, align_bytes=64)
+        last_bf = turns.tile([P, P, PACK], BF16, name="last_bf", offset=0, align_bytes=64)
         nc.vector.tensor_copy(out=early_bf[:].rearrange("p j m r -> p m r j"), in_=source[:, :, :, 0:EARLY])
         nc.scalar.copy(out=last_bf[:], in_=source[:, :, :, EARLY])
 
@@ -115,6 +112,16 @@ def tile_attend_headwrite_kernel(tc, emb_words, emb_scales, wv, old, retain, off
             in_=last_bf[:].rearrange("p m r -> p (m r)"),
         )
 
+        old_view = old.rearrange("(p j) t -> p j t", j=TILES)
+        out_view = out.rearrange("(p j) t -> p j t", j=TILES)
+        halves = [slice(h * BANK, (h + 1) * BANK) for h in range(HALVES)]
+        old_all = turns.tile([P, TILES * T], F32, name="old_all", offset=OLD_OFFSET, align_bytes=64)
+        old_sb = [old_all[:, j * T : (j + 1) * T] for j in range(TILES)]
+        for cols in halves:
+            nc.sync.dma_start(out=old_sb[0][:, cols], in_=old_view[:, 0, cols])
+        for j in range(1, TILES):
+            nc.sync.dma_start(out=old_sb[j], in_=old_view[:, j, :])
+
         retain_all = keep.tile([P, T], F32, name="retain_all", tag="wv_raw")
         for h in range(HALVES):
             for c in range(PER_BANK):
@@ -122,9 +129,9 @@ def tile_attend_headwrite_kernel(tc, emb_words, emb_scales, wv, old, retain, off
                 nc.tensor.transpose(
                     banks[5 + h][:, c * P : (c + 1) * P], retain_cols[:, b : b + 1].to_broadcast([P, P]), ident[:]
                 )
-            nc.scalar.copy(retain_all[:, h * BANK : (h + 1) * BANK], banks[5 + h][:])
+            nc.scalar.copy(retain_all[:, halves[h]], banks[5 + h][:])
 
-        picked_words = turns.tile([P, I], U32, name="picked_words", offset=0, align_bytes=64)
+        picked_words = turns.tile([P, I], U32, name="picked_words", offset=EARLY_OFFSET, align_bytes=64)
         for lo, hi in ((0, FIRST), (FIRST, I)):
             nc.vector.tensor_copy(picked_words[:, lo:hi], words[:].indirect(emb_list[:, lo // 16 : hi // 16]))
 
@@ -147,10 +154,11 @@ def tile_attend_headwrite_kernel(tc, emb_words, emb_scales, wv, old, retain, off
         for j, lo, hi in pieces[:-1]:
             nc.vector.tensor_copy(windows[j][:].indirect(place_list[:, lo // 16 : hi // 16]), values[j][:, lo:hi])
 
-        kept = [turns.tile([P, T], F32, name="kept0", offset=LAST_OFFSET, align_bytes=64)]
+        kept = [turns.tile([P, T], F32, name="kept0", offset=0, align_bytes=64)]
         kept.extend(keep.tile([P, T], F32, name="kept%d" % j, tag="kept%d" % j) for j in range(1, 3))
-        for j in range(2):
-            nc.gpsimd.tensor_tensor(kept[j][:], old_sb[j][:], retain_all[:], MULT)
+        for cols in halves:
+            nc.gpsimd.tensor_tensor(kept[0][:, cols], old_sb[0][:, cols], retain_all[:, cols], MULT)
+        nc.gpsimd.tensor_tensor(kept[1][:], old_sb[1], retain_all[:], MULT)
 
         kept_t = [keep.tile([P, 2, P], F32, name="kept_t%d" % b) for b in range(BLOCKS)]
         for b in range(BLOCKS):
@@ -166,25 +174,23 @@ def tile_attend_headwrite_kernel(tc, emb_words, emb_scales, wv, old, retain, off
                     nc.tensor.transpose(
                         banks[2 * j + h][:, c * P : (c + 1) * P], kept_t[h * PER_BANK + c][:, j, :], ident[:]
                     )
-        kept_last = keep.tile([P, 256], F32, name="kept_last")
-        nc.scalar.copy(kept_last[:, 0:192], banks[2][:, 320:])
-        nc.scalar.copy(kept_last[:, 192:], banks[3][:, 0:64])
+        kept_last = keep.tile([P, SHARE], F32, name="kept_last")
+        nc.scalar.copy(kept_last[:], banks[3][:, BANK - SHARE :])
         for h in range(HALVES):
-            nc.scalar.copy(kept[2][:, h * BANK : (h + 1) * BANK], banks[h][:])
+            nc.scalar.copy(kept[2][:, halves[h]], banks[h][:])
 
         for j in range(2):
             result = old_sb[1 - j]
-            nc.gpsimd.tensor_tensor(result[:], kept[j][:], windows[j][:], ADD)
-            nc.sync.dma_start(out=out_view[:, j, :], in_=result[:])
+            nc.gpsimd.tensor_tensor(result, kept[j][:], windows[j][:], ADD)
+            nc.sync.dma_start(out=out_view[:, j, :], in_=result)
         nc.vector.tensor_copy(windows[0][:].indirect(place_list[:]), values[3][:])
-        for h in range(HALVES):
-            cols = slice(h * BANK, (h + 1) * BANK)
+        for cols in halves:
             nc.gpsimd.tensor_tensor(old_sb[2][:, cols], kept[2][:, cols], windows[2][:, cols], ADD)
             nc.scalar.dma_start(out=out_view[:, 2, cols], in_=old_sb[2][:, cols])
 
         sums = keep.tile([P, T], F32, name="sums", tag="kept2")
-        nc.gpsimd.tensor_tensor(sums[:, 320:576], kept_last[:], windows[0][:, 320:576], ADD)
-        for start, lo, hi in ((0, 0, 128), (128, 128, 320), (320, 576, 704), (704, 704, 1024)):
+        nc.gpsimd.tensor_tensor(sums[:, T - SHARE :], kept_last[:], windows[0][:, T - SHARE :], ADD)
+        for lo, hi, end in ((0, 128, 128), (128, 256, 256), (256, 512, 512), (512, T - SHARE, T)):
             h, col = divmod(lo, BANK)
             nc.vector.tensor_tensor(sums[:, lo:hi], banks[2 + h][:, col : col + hi - lo], windows[0][:, lo:hi], ADD)
-            nc.sync.dma_start(out=out_view[:, 3, start:hi], in_=sums[:, start:hi])
+            nc.sync.dma_start(out=out_view[:, 3, lo:end], in_=sums[:, lo:end])

@@ -24,13 +24,14 @@ BLOCKS = T // P
 HALVES = T // BANK
 PER_BANK = BANK // P
 SCALE_ROWS = 16
-SPREAD = P // SCALE_ROWS
+ROW_FIRST = 11
+ROW_STEP = 7
 FIRST = 128
 WV_FIRST = 768
-EARLY = 3
-SHARE = 256
-EARLY_OFFSET = T * 4
-OLD_OFFSET = EARLY_OFFSET + I * 4
+EARLY = 2
+PICKED_OFFSET = T * 4
+EARLY_OFFSET = PICKED_OFFSET + 64
+OLD_OFFSET = PICKED_OFFSET + I * 4
 
 
 def tile_attend_headwrite_kernel(tc, emb_words, emb_scales, wv, old, retain, offs, offs2, out):
@@ -64,15 +65,17 @@ def tile_attend_headwrite_kernel(tc, emb_words, emb_scales, wv, old, retain, off
         word_rows = emb_words[0].rearrange("p n r -> p (n r)").bitcast(I32)
         nc.sync.dma_start(out=wv_flat[:, 0:WV_FIRST], in_=wv_rows[:, 0:WV_FIRST])
         nc.sync.dma_start(emb_list[:], offs)
-        nc.sync.dma_start(out=scales[0:P:SPREAD, :].bitcast(I32), in_=emb_scales[0].bitcast(I32))
+        nc.sync.dma_start(out=scales[ROW_FIRST : ROW_FIRST + SCALE_ROWS * ROW_STEP : ROW_STEP, :].bitcast(I32), in_=emb_scales[0].bitcast(I32))
         nc.sync.dma_start(out=retain_rows[0:BLOCKS, :], in_=retain.rearrange("o (b q) -> (o b) q", q=P))
         nc.sync.dma_start(out=wv_flat[:, WV_FIRST:], in_=wv_rows[:, WV_FIRST:])
         nc.sync.dma_start(out=words[:].bitcast(I32), in_=word_rows)
 
         nc.vector.tensor_copy(picked_scales[:], scales[:].indirect(emb_list[:]))
         for r in range(4):
+            start = ROW_FIRST + r * ROW_STEP
             nc.sync.dma_start(
-                out=plane[r:P:32, :].bitcast(I32), in_=picked_scales[r * SPREAD : P : 32, :].bitcast(I32)
+                out=plane[r:P:32, :].bitcast(I32),
+                in_=picked_scales[start : start + 13 * ROW_STEP : 4 * ROW_STEP, :].bitcast(I32),
             )
         nc.sync.dma_start(place_list[:], offs2)
 
@@ -95,9 +98,9 @@ def tile_attend_headwrite_kernel(tc, emb_words, emb_scales, wv, old, retain, off
 
         source = wv_raw[:].rearrange("p r (m j) -> p m r j", j=TILES)
         early_bf = turns.tile([P, EARLY, P, PACK], BF16, name="early_bf", offset=EARLY_OFFSET, align_bytes=64)
-        last_bf = turns.tile([P, P, PACK], BF16, name="last_bf", offset=0, align_bytes=64)
+        last_bf = turns.tile([P, TILES - EARLY, P, PACK], BF16, name="last_bf", offset=0, align_bytes=64)
         nc.vector.tensor_copy(out=early_bf[:].rearrange("p j m r -> p m r j"), in_=source[:, :, :, 0:EARLY])
-        nc.scalar.copy(out=last_bf[:], in_=source[:, :, :, EARLY])
+        nc.scalar.copy(out=last_bf[:].rearrange("p j m r -> p m r j"), in_=source[:, :, :, EARLY:])
 
         wv_codes = keep.tile([P, E], U32, name="wv_codes", align_bytes=64)
         wv_scales = keep.tile([P, E], U8, name="wv_scales", align_bytes=64)
@@ -109,7 +112,7 @@ def tile_attend_headwrite_kernel(tc, emb_words, emb_scales, wv, old, retain, off
         nc.vector.quantize_mx(
             out=wv_codes[:, EARLY * P :].bitcast(FP8X4),
             scales=wv_scales[:, EARLY * P :],
-            in_=last_bf[:].rearrange("p m r -> p (m r)"),
+            in_=last_bf[:].rearrange("p j m r -> p (j m r)"),
         )
 
         old_view = old.rearrange("(p j) t -> p j t", j=TILES)
@@ -131,7 +134,7 @@ def tile_attend_headwrite_kernel(tc, emb_words, emb_scales, wv, old, retain, off
                 )
             nc.scalar.copy(retain_all[:, halves[h]], banks[5 + h][:])
 
-        picked_words = turns.tile([P, I], U32, name="picked_words", offset=EARLY_OFFSET, align_bytes=64)
+        picked_words = turns.tile([P, I], U32, name="picked_words", offset=PICKED_OFFSET, align_bytes=64)
         for lo, hi in ((0, FIRST), (FIRST, I)):
             nc.vector.tensor_copy(picked_words[:, lo:hi], words[:].indirect(emb_list[:, lo // 16 : hi // 16]))
 
@@ -174,8 +177,9 @@ def tile_attend_headwrite_kernel(tc, emb_words, emb_scales, wv, old, retain, off
                     nc.tensor.transpose(
                         banks[2 * j + h][:, c * P : (c + 1) * P], kept_t[h * PER_BANK + c][:, j, :], ident[:]
                     )
-        kept_last = keep.tile([P, SHARE], F32, name="kept_last")
-        nc.scalar.copy(kept_last[:], banks[3][:, BANK - SHARE :])
+        kept_last = keep.tile([P, 256], F32, name="kept_last")
+        nc.scalar.copy(kept_last[:, 0:192], banks[2][:, 320:])
+        nc.scalar.copy(kept_last[:, 192:], banks[3][:, 0:64])
         for h in range(HALVES):
             nc.scalar.copy(kept[2][:, halves[h]], banks[h][:])
 
@@ -186,11 +190,11 @@ def tile_attend_headwrite_kernel(tc, emb_words, emb_scales, wv, old, retain, off
         nc.vector.tensor_copy(windows[0][:].indirect(place_list[:]), values[3][:])
         for cols in halves:
             nc.gpsimd.tensor_tensor(old_sb[2][:, cols], kept[2][:, cols], windows[2][:, cols], ADD)
-            nc.scalar.dma_start(out=out_view[:, 2, cols], in_=old_sb[2][:, cols])
+            nc.sync.dma_start(out=out_view[:, 2, cols], in_=old_sb[2][:, cols])
 
         sums = keep.tile([P, T], F32, name="sums", tag="kept2")
-        nc.gpsimd.tensor_tensor(sums[:, T - SHARE :], kept_last[:], windows[0][:, T - SHARE :], ADD)
-        for lo, hi, end in ((0, 128, 128), (128, 256, 256), (256, 512, 512), (512, T - SHARE, T)):
+        nc.gpsimd.tensor_tensor(sums[:, 320:576], kept_last[:], windows[0][:, 320:576], ADD)
+        for start, lo, hi in ((0, 0, 128), (128, 128, 320), (320, 576, 704), (704, 704, 1024)):
             h, col = divmod(lo, BANK)
             nc.vector.tensor_tensor(sums[:, lo:hi], banks[2 + h][:, col : col + hi - lo], windows[0][:, lo:hi], ADD)
-            nc.sync.dma_start(out=out_view[:, 3, lo:end], in_=sums[:, lo:end])
+            nc.sync.dma_start(out=out_view[:, 3, start:hi], in_=sums[:, start:hi])

@@ -29,8 +29,8 @@ ROW_STEP = 7
 FIRST = 128
 WV_FIRST = 768
 EARLY = 2
-PICKED_OFFSET = T * 4
-EARLY_OFFSET = PICKED_OFFSET + 64
+EARLY_OFFSET = (TILES - EARLY) * P * PACK * 2
+PICKED_OFFSET = EARLY_OFFSET - 64
 OLD_OFFSET = PICKED_OFFSET + I * 4
 
 
@@ -53,7 +53,7 @@ def tile_attend_headwrite_kernel(tc, emb_words, emb_scales, wv, old, retain, off
         plane = keep.tile([P, I], U8, name="plane", align_bytes=64)
 
         nc.vector.memset(scales[:].bitcast(I32), 0)
-        nc.vector.memset(retain_rows[:], 0.0)
+        nc.vector.memset(retain_rows[0 : P - BLOCKS, :], 0.0)
         windows = [keep.tile([P, T], F32, name="window%d" % j) for j in range(2)]
         for window in windows:
             nc.vector.memset(window[:].bitcast(I32), 0)
@@ -66,7 +66,7 @@ def tile_attend_headwrite_kernel(tc, emb_words, emb_scales, wv, old, retain, off
         nc.sync.dma_start(out=wv_flat[:, 0:WV_FIRST], in_=wv_rows[:, 0:WV_FIRST])
         nc.sync.dma_start(emb_list[:], offs)
         nc.sync.dma_start(out=scales[ROW_FIRST : ROW_FIRST + SCALE_ROWS * ROW_STEP : ROW_STEP, :].bitcast(I32), in_=emb_scales[0].bitcast(I32))
-        nc.sync.dma_start(out=retain_rows[0:BLOCKS, :], in_=retain.rearrange("o (b q) -> (o b) q", q=P))
+        nc.scalar.dma_start(out=retain_rows[P - BLOCKS :, :], in_=retain.rearrange("o (b q) -> (o b) q", q=P))
         nc.sync.dma_start(out=wv_flat[:, WV_FIRST:], in_=wv_rows[:, WV_FIRST:])
         nc.sync.dma_start(out=words[:].bitcast(I32), in_=word_rows)
 
@@ -94,7 +94,7 @@ def tile_attend_headwrite_kernel(tc, emb_words, emb_scales, wv, old, retain, off
 
         retain_cols = keep.tile([P, BLOCKS], F32, name="retain_cols")
         nc.tensor.transpose(banks[7][:, 0:P], retain_rows[:], ident[:])
-        nc.scalar.copy(retain_cols[:], banks[7][:, 0:BLOCKS])
+        nc.scalar.copy(retain_cols[:], banks[7][:, P - BLOCKS : P])
 
         source = wv_raw[:].rearrange("p r (m j) -> p m r j", j=TILES)
         early_bf = turns.tile([P, EARLY, P, PACK], BF16, name="early_bf", offset=EARLY_OFFSET, align_bytes=64)
@@ -157,8 +157,7 @@ def tile_attend_headwrite_kernel(tc, emb_words, emb_scales, wv, old, retain, off
         for j, lo, hi in pieces[:-1]:
             nc.vector.tensor_copy(windows[j][:].indirect(place_list[:, lo // 16 : hi // 16]), values[j][:, lo:hi])
 
-        kept = [turns.tile([P, T], F32, name="kept0", offset=0, align_bytes=64)]
-        kept.extend(keep.tile([P, T], F32, name="kept%d" % j, tag="kept%d" % j) for j in range(1, 3))
+        kept = [keep.tile([P, T], F32, name="kept%d" % j, tag="kept%d" % j) for j in range(3)]
         for cols in halves:
             nc.gpsimd.tensor_tensor(kept[0][:, cols], old_sb[0][:, cols], retain_all[:, cols], MULT)
         nc.gpsimd.tensor_tensor(kept[1][:], old_sb[1], retain_all[:], MULT)

@@ -28,10 +28,12 @@ ROW_FIRST = 11
 ROW_STEP = 7
 FIRST = 128
 WV_FIRST = 768
-EARLY = 2
-EARLY_OFFSET = (TILES - EARLY) * P * PACK * 2
-PICKED_OFFSET = EARLY_OFFSET - 64
-OLD_OFFSET = PICKED_OFFSET + I * 4
+SPLIT = 72
+TILE_BYTES = P * PACK * 2
+RETAIN_OFFSET = U
+RAW_OFFSET = TILES * TILE_BYTES
+PICKED_OFFSET = RAW_OFFSET + T * 4
+OLD_OFFSET = RAW_OFFSET + PACK * E * 4 - 64
 
 
 def tile_attend_headwrite_kernel(tc, emb_words, emb_scales, wv, old, retain, offs, offs2, out):
@@ -44,10 +46,10 @@ def tile_attend_headwrite_kernel(tc, emb_words, emb_scales, wv, old, retain, off
 
         emb_list = keep.tile([P, I // 16], U16, name="emb_list")
         place_list = keep.tile([P, I // 16], U16, name="place_list")
-        wv_raw = keep.tile([P, PACK, E], F32, name="wv_raw", tag="wv_raw")
+        wv_raw = turns.tile([P, PACK, E], F32, name="wv_raw", offset=RAW_OFFSET, align_bytes=64)
         words = keep.tile([P, U], U32, name="words")
-        scales = turns.tile([P, U], U8, name="scales", offset=EARLY_OFFSET, align_bytes=64)
-        retain_rows = turns.tile([P, P], F32, name="retain_rows", offset=0, align_bytes=64)
+        scales = turns.tile([P, U], U8, name="scales", offset=0, align_bytes=64)
+        retain_rows = turns.tile([P, P], F32, name="retain_rows", offset=RETAIN_OFFSET, align_bytes=64)
         ident = keep.tile([P, P], F32, name="ident")
         picked_scales = keep.tile([P, I], U8, name="picked_scales", align_bytes=64)
         plane = keep.tile([P, I], U8, name="plane", align_bytes=64)
@@ -97,22 +99,17 @@ def tile_attend_headwrite_kernel(tc, emb_words, emb_scales, wv, old, retain, off
         nc.scalar.copy(retain_cols[:], banks[7][:, P - BLOCKS : P])
 
         source = wv_raw[:].rearrange("p r (m j) -> p m r j", j=TILES)
-        early_bf = turns.tile([P, EARLY, P, PACK], BF16, name="early_bf", offset=EARLY_OFFSET, align_bytes=64)
-        last_bf = turns.tile([P, TILES - EARLY, P, PACK], BF16, name="last_bf", offset=0, align_bytes=64)
-        nc.vector.tensor_copy(out=early_bf[:].rearrange("p j m r -> p m r j"), in_=source[:, :, :, 0:EARLY])
-        nc.scalar.copy(out=last_bf[:].rearrange("p j m r -> p m r j"), in_=source[:, :, :, EARLY:])
+        wv_bf = turns.tile([P, TILES, P, PACK], BF16, name="wv_bf", offset=0, align_bytes=64)
+        laid = wv_bf[:].rearrange("p j m r -> p m r j")
+        nc.vector.tensor_copy(out=laid[:, 0:SPLIT], in_=source[:, 0:SPLIT])
+        nc.scalar.copy(out=laid[:, SPLIT:], in_=source[:, SPLIT:])
 
         wv_codes = keep.tile([P, E], U32, name="wv_codes", align_bytes=64)
         wv_scales = keep.tile([P, E], U8, name="wv_scales", align_bytes=64)
         nc.vector.quantize_mx(
-            out=wv_codes[:, 0 : EARLY * P].bitcast(FP8X4),
-            scales=wv_scales[:, 0 : EARLY * P],
-            in_=early_bf[:].rearrange("p j m r -> p (j m r)"),
-        )
-        nc.vector.quantize_mx(
-            out=wv_codes[:, EARLY * P :].bitcast(FP8X4),
-            scales=wv_scales[:, EARLY * P :],
-            in_=last_bf[:].rearrange("p j m r -> p (j m r)"),
+            out=wv_codes[:].bitcast(FP8X4),
+            scales=wv_scales[:],
+            in_=wv_bf[:].rearrange("p j m r -> p (j m r)"),
         )
 
         old_view = old.rearrange("(p j) t -> p j t", j=TILES)
@@ -125,7 +122,7 @@ def tile_attend_headwrite_kernel(tc, emb_words, emb_scales, wv, old, retain, off
         for j in range(1, TILES):
             nc.sync.dma_start(out=old_sb[j], in_=old_view[:, j, :])
 
-        retain_all = keep.tile([P, T], F32, name="retain_all", tag="wv_raw")
+        retain_all = turns.tile([P, T], F32, name="retain_all", offset=RAW_OFFSET, align_bytes=64)
         for h in range(HALVES):
             for c in range(PER_BANK):
                 b = h * PER_BANK + c

@@ -30,10 +30,12 @@ FIRST = 128
 WV_FIRST = 768
 SPLIT = 72
 TILE_BYTES = P * PACK * 2
-RETAIN_OFFSET = U
-RAW_OFFSET = TILES * TILE_BYTES
+RAW_OFFSET = 0
 PICKED_OFFSET = RAW_OFFSET + T * 4
-OLD_OFFSET = RAW_OFFSET + PACK * E * 4 - 64
+LAID_OFFSET = RAW_OFFSET + PACK * E * 4
+RETAIN_OFFSET = LAID_OFFSET
+SCALES_OFFSET = LAID_OFFSET + TILES * TILE_BYTES - U // 2
+OLD_OFFSET = SCALES_OFFSET + U - 64
 
 
 def tile_attend_headwrite_kernel(tc, emb_words, emb_scales, wv, old, retain, offs, offs2, out):
@@ -48,7 +50,7 @@ def tile_attend_headwrite_kernel(tc, emb_words, emb_scales, wv, old, retain, off
         place_list = keep.tile([P, I // 16], U16, name="place_list")
         wv_raw = turns.tile([P, PACK, E], F32, name="wv_raw", offset=RAW_OFFSET, align_bytes=64)
         words = keep.tile([P, U], U32, name="words")
-        scales = turns.tile([P, U], U8, name="scales", offset=0, align_bytes=64)
+        scales = turns.tile([P, U], U8, name="scales", offset=SCALES_OFFSET, align_bytes=64)
         retain_rows = turns.tile([P, P], F32, name="retain_rows", offset=RETAIN_OFFSET, align_bytes=64)
         ident = keep.tile([P, P], F32, name="ident")
         picked_scales = keep.tile([P, I], U8, name="picked_scales", align_bytes=64)
@@ -99,7 +101,7 @@ def tile_attend_headwrite_kernel(tc, emb_words, emb_scales, wv, old, retain, off
         nc.scalar.copy(retain_cols[:], banks[7][:, P - BLOCKS : P])
 
         source = wv_raw[:].rearrange("p r (m j) -> p m r j", j=TILES)
-        wv_bf = turns.tile([P, TILES, P, PACK], BF16, name="wv_bf", offset=0, align_bytes=64)
+        wv_bf = turns.tile([P, TILES, P, PACK], BF16, name="wv_bf", offset=LAID_OFFSET, align_bytes=64)
         laid = wv_bf[:].rearrange("p j m r -> p m r j")
         nc.vector.tensor_copy(out=laid[:, 0:SPLIT], in_=source[:, 0:SPLIT])
         nc.scalar.copy(out=laid[:, SPLIT:], in_=source[:, SPLIT:])

from contextlib import ExitStack

import concourse.mybir as mybir

K, U, I, T, E = 512, 2048, 512, 1024, 512
FLOPS = 2 * K * E * I

F32 = mybir.dt.float32
BF16 = mybir.dt.bfloat16
I32 = mybir.dt.int32
U32 = mybir.dt.uint32
U16 = mybir.dt.uint16
U8 = mybir.dt.uint8
FP8X4 = mybir.dt.float8_e4m3fn_x4
COPY = mybir.ActivationFunctionType.Copy
ADD = mybir.AluOpType.add
MULT = mybir.AluOpType.mult

P = 128
PACK = 4
TILES = E // P
BANK = 512
BLOCKS = T // P
HALVES = T // BANK
PER_BANK = BANK // P
SCALE_ROWS = 16
ROW_FIRST = 11
ROW_STEP = 7
FIRST = 128
WV_FIRST = 768
SPLIT = 72
TILE_BYTES = P * PACK * 2
RAW_OFFSET = 0
PICKED_OFFSET = RAW_OFFSET + T * 4
LAID_OFFSET = RAW_OFFSET + PACK * E * 4
RETAIN_OFFSET = LAID_OFFSET
SCALES_OFFSET = LAID_OFFSET + TILES * TILE_BYTES - U // 2
OLD_OFFSET = SCALES_OFFSET + U - 64


def tile_attend_headwrite_kernel(tc, emb_words, emb_scales, wv, old, retain, offs, offs2, out):
    nc = tc.nc
    with ExitStack() as ctx:
        keep = ctx.enter_context(tc.tile_pool(name="keep", bufs=1))
        turns = ctx.enter_context(tc.tile_pool(name="turns", bufs=1))
        psum = ctx.enter_context(tc.psum_pool(name="psum", bufs=1))
        banks = [psum.tile([P, BANK], F32, name="bank%d" % n) for n in range(8)]

        emb_list = keep.tile([P, I // 16], U16, name="emb_list")
        place_list = keep.tile([P, I // 16], U16, name="place_list")
        wv_raw = turns.tile([P, PACK, E], F32, name="wv_raw", offset=RAW_OFFSET, align_bytes=64)
        words = keep.tile([P, U], U32, name="words")
        scales = turns.tile([P, U], U8, name="scales", offset=SCALES_OFFSET, align_bytes=64)
        retain_rows = turns.tile([P, P], F32, name="retain_rows", offset=RETAIN_OFFSET, align_bytes=64)
        ident = keep.tile([P, P], F32, name="ident")
        picked_scales = keep.tile([P, I], U8, name="picked_scales", align_bytes=64)
        plane = keep.tile([P, I], U8, name="plane", align_bytes=64)

        nc.vector.memset(scales[:].bitcast(I32), 0)
        nc.vector.memset(retain_rows[0 : P - BLOCKS, :], 0.0)
        windows = [keep.tile([P, T], F32, name="window%d" % j) for j in range(2)]
        for window in windows:
            nc.vector.memset(window[:].bitcast(I32), 0)
        zeros = keep.tile([P, P], F32, name="zeros", tag="window2")
        nc.vector.memset(zeros[:], 0.0)

        wv_rows = wv.rearrange("(p r) e -> p (r e)", r=PACK)
        wv_flat = wv_raw[:].rearrange("p r e -> p (r e)")
        word_rows = emb_words[0].rearrange("p n r -> p (n r)").bitcast(I32)
        nc.sync.dma_start(out=wv_flat[:, 0:WV_FIRST], in_=wv_rows[:, 0:WV_FIRST])
        nc.sync.dma_start(emb_list[:], offs)
        nc.sync.dma_start(out=scales[ROW_FIRST : ROW_FIRST + SCALE_ROWS * ROW_STEP : ROW_STEP, :].bitcast(I32), in_=emb_scales[0].bitcast(I32))
        nc.scalar.dma_start(out=retain_rows[P - BLOCKS :, :], in_=retain.rearrange("o (b q) -> (o b) q", q=P))
        nc.sync.dma_start(out=wv_flat[:, WV_FIRST:], in_=wv_rows[:, WV_FIRST:])
        nc.sync.dma_start(out=words[:].bitcast(I32), in_=word_rows)

        nc.vector.tensor_copy(picked_scales[:], scales[:].indirect(emb_list[:]))
        for r in range(4):
            start = ROW_FIRST + r * ROW_STEP
            nc.sync.dma_start(
                out=plane[r:P:32, :].bitcast(I32),
                in_=picked_scales[start : start + 13 * ROW_STEP : 4 * ROW_STEP, :].bitcast(I32),
            )
        nc.sync.dma_start(place_list[:], offs2)

        nc.gpsimd.affine_select(
            out=ident[:],
            in_=zeros[:],
            compare_op=mybir.AluOpType.not_equal,
            fill=1.0,
            base=0,
            pattern=[[-1, P]],
            channel_multiplier=1,
        )

        windows.append(keep.tile([P, T], F32, name="window2", tag="window2"))
        nc.gpsimd.memset(windows[2][:], 0.0)

        retain_cols = keep.tile([P, BLOCKS], F32, name="retain_cols")
        nc.tensor.transpose(banks[7][:, 0:P], retain_rows[:], ident[:])
        nc.scalar.copy(retain_cols[:], banks[7][:, P - BLOCKS : P])

        source = wv_raw[:].rearrange("p r (m j) -> p m r j", j=TILES)
        wv_bf = turns.tile([P, TILES, P, PACK], BF16, name="wv_bf", offset=LAID_OFFSET, align_bytes=64)
        laid = wv_bf[:].rearrange("p j m r -> p m r j")
        nc.vector.tensor_copy(out=laid[:, 0:SPLIT], in_=source[:, 0:SPLIT])
        nc.scalar.copy(out=laid[:, SPLIT:], in_=source[:, SPLIT:])

        wv_codes = keep.tile([P, E], U32, name="wv_codes", align_bytes=64)
        wv_scales = keep.tile([P, E], U8, name="wv_scales", align_bytes=64)
        nc.vector.quantize_mx(
            out=wv_codes[:].bitcast(FP8X4),
            scales=wv_scales[:],
            in_=wv_bf[:].rearrange("p j m r -> p (j m r)"),
        )

        old_view = old.rearrange("(p j) t -> p j t", j=TILES)
        out_view = out.rearrange("(p j) t -> p j t", j=TILES)
        halves = [slice(h * BANK, (h + 1) * BANK) for h in range(HALVES)]
        old_all = turns.tile([P, TILES * T], F32, name="old_all", offset=OLD_OFFSET, align_bytes=64)
        old_sb = [old_all[:, j * T : (j + 1) * T] for j in range(TILES)]
        for cols in halves:
            nc.sync.dma_start(out=old_sb[0][:, cols], in_=old_view[:, 0, cols])
        for j in range(1, TILES):
            nc.sync.dma_start(out=old_sb[j], in_=old_view[:, j, :])

        retain_all = turns.tile([P, T], F32, name="retain_all", offset=RAW_OFFSET, align_bytes=64)
        for h in range(HALVES):
            for c in range(PER_BANK):
                b = h * PER_BANK + c
                nc.tensor.transpose(
                    banks[5 + h][:, c * P : (c + 1) * P], retain_cols[:, b : b + 1].to_broadcast([P, P]), ident[:]
                )
            nc.scalar.copy(retain_all[:, halves[h]], banks[5 + h][:])

        picked_words = turns.tile([P, I], U32, name="picked_words", offset=PICKED_OFFSET, align_bytes=64)
        for lo, hi in ((0, FIRST), (FIRST, I)):
            nc.vector.tensor_copy(picked_words[:, lo:hi], words[:].indirect(emb_list[:, lo // 16 : hi // 16]))

        pieces = [(0, 0, FIRST), (1, 0, FIRST), (0, FIRST, I), (1, FIRST, I), (2, 0, I), (3, 0, I)]
        product_banks = [banks[n] for n in (0, 1, 2, 3, 4, 7)]
        values = [keep.tile([P, I], F32, name="values%d" % j) for j in range(TILES)]
        for n, (j, lo, hi) in enumerate(pieces):
            cuts = [lo, 2 * FIRST, hi] if lo == FIRST else [lo, hi]
            for a, b in zip(cuts, cuts[1:]):
                nc.tensor.matmul_mx(
                    out=product_banks[n][:, a - lo : b - lo],
                    lhsT=wv_codes[:, j * P : (j + 1) * P].bitcast(FP8X4),
                    lhsT_scale=wv_scales[:, j * P : (j + 1) * P],
                    rhs=picked_words[:, a:b].bitcast(FP8X4),
                    rhs_scale=plane[:, a:b],
                    start=True,
                    stop=True,
                )
            nc.scalar.copy(values[j][:, lo:hi], product_banks[n][:, 0 : hi - lo])
        for j, lo, hi in pieces[:-1]:
            nc.vector.tensor_copy(windows[j][:].indirect(place_list[:, lo // 16 : hi // 16]), values[j][:, lo:hi])

        kept = [keep.tile([P, T], F32, name="kept%d" % j, tag="kept%d" % j) for j in range(3)]
        for cols in halves:
            nc.gpsimd.tensor_tensor(kept[0][:, cols], old_sb[0][:, cols], retain_all[:, cols], MULT)
        nc.gpsimd.tensor_tensor(kept[1][:], old_sb[1], retain_all[:], MULT)

        kept_t = [keep.tile([P, 2, P], F32, name="kept_t%d" % b) for b in range(BLOCKS)]
        for b in range(BLOCKS):
            bank = banks[4 + b % 4]
            for j in range(2):
                nc.tensor.transpose(bank[:, j * P : (j + 1) * P], old_sb[2 + j][:, b * P : (b + 1) * P], ident[:])
            nc.scalar.activation(
                kept_t[b][:].rearrange("q j p -> q (j p)"), bank[:, 0 : 2 * P], COPY, scale=retain_cols[:, b : b + 1]
            )
        for j in (1, 0):
            for h in range(HALVES):
                for c in range(PER_BANK):
                    nc.tensor.transpose(
                        banks[2 * j + h][:, c * P : (c + 1) * P], kept_t[h * PER_BANK + c][:, j, :], ident[:]
                    )
        kept_last = keep.tile([P, 256], F32, name="kept_last")
        nc.scalar.copy(kept_last[:, 0:192], banks[2][:, 320:])
        nc.scalar.copy(kept_last[:, 192:], banks[3][:, 0:64])
        for h in range(HALVES):
            nc.scalar.copy(kept[2][:, halves[h]], banks[h][:])

        for j in range(2):
            result = old_sb[1 - j]
            nc.gpsimd.tensor_tensor(result, kept[j][:], windows[j][:], ADD)
            nc.sync.dma_start(out=out_view[:, j, :], in_=result)
        nc.vector.tensor_copy(windows[0][:].indirect(place_list[:]), values[3][:])
        for cols in halves:
            nc.gpsimd.tensor_tensor(old_sb[2][:, cols], kept[2][:, cols], windows[2][:, cols], ADD)
            nc.sync.dma_start(out=out_view[:, 2, cols], in_=old_sb[2][:, cols])

        sums = keep.tile([P, T], F32, name="sums", tag="kept2")
        nc.gpsimd.tensor_tensor(sums[:, 320:576], kept_last[:], windows[0][:, 320:576], ADD)
        for start, lo, hi in ((0, 0, 128), (128, 128, 320), (320, 576, 704), (704, 704, 1024)):
            h, col = divmod(lo, BANK)
            nc.vector.tensor_tensor(sums[:, lo:hi], banks[2 + h][:, col : col + hi - lo], windows[0][:, lo:hi], ADD)
            nc.sync.dma_start(out=out_view[:, 3, start:hi], in_=sums[:, start:hi])
